import numpy as np
import ml_dtypes


def mxq(x, axis, fmt="e4m3"):
    dtype, down = {"e4m3": (ml_dtypes.float8_e4m3fn, 7), "e5m2": (ml_dtypes.float8_e5m2, 14)}[fmt]
    v = np.moveaxis(np.asarray(x, np.float32).astype(ml_dtypes.bfloat16).astype(np.float64), axis, -1)
    blocks = v.reshape(v.shape[:-1] + (-1, 32))
    amax = np.abs(blocks).max(-1, keepdims=True)
    byte = np.maximum(np.where(amax > 0, np.frexp(amax)[1] - 1 + 127, 0) - down, 1)
    scale = np.exp2(byte - 127.0)
    codes = (blocks / scale).astype(np.float32).astype(dtype).astype(np.float64)
    return np.moveaxis((codes * scale).reshape(v.shape), -1, axis)


WIDE = False


def mx_kscale(k):
    if not WIDE:
        return np.ones(k)
    levels = np.array([10, -10, 5, -5, 0])
    if k % 512:
        return np.exp2(np.random.permutation(np.resize(levels, k // 32))).repeat(32)
    a = np.empty((k // 512, 16))
    for p in range(k // 512):
        a[p, :8] = np.random.permutation(np.resize(levels, 8))
        for g in range(8):
            far = levels[np.abs(levels - a[p, g]) >= 10]
            a[p, g + 8] = far[np.random.randint(len(far))]
    return np.exp2(a.ravel()).repeat(32)


def f64(x):
    return np.asarray(x).astype(np.float64)


def striped(idx):
    return np.tile(idx.reshape(-1, 16).T, (8, 1)).astype(np.uint16)


def unstriped(offs):
    return offs[:16].T.reshape(-1).astype(np.int64)


def striped8(idx):
    return np.concatenate([x.reshape(-1, 16).T for x in idx]).astype(np.uint16)


def runs(offs, k):
    lists = np.stack([offs[16 * r : 16 * r + 16].T.reshape(-1) for r in range(8)]).astype(np.int64)
    return lists[np.arange(k) % 512 // 64]


def pack_weight(w):
    k, n = w.shape
    w = f64(np.asarray(w, np.float32).astype(ml_dtypes.bfloat16)).reshape(k // 32, 32, n)
    amax = np.abs(w).max(1)
    byte = np.clip(np.where(amax > 0, np.frexp(amax)[1] - 1 + 127 - 7, 1), 1, 254)
    scaled = (w * np.exp2(127.0 - byte)[:, None, :]).reshape(k, n).astype(np.float32)
    words = np.ascontiguousarray(scaled.reshape(k // 512, 128, 4, n).transpose(0, 1, 3, 2)).astype(ml_dtypes.float8_e4m3fn).view(np.uint8)
    return words, np.ascontiguousarray(byte.astype(np.uint8).reshape(k // 512, 16, n))


def unpack_weight(words, scales):
    g, p, n, _ = words.shape
    vals = np.ascontiguousarray(words).view(ml_dtypes.float8_e4m3fn).astype(np.float64) * np.repeat(np.exp2(scales.astype(np.float64) - 127.0), 8, axis=1)[..., None]
    return vals.transpose(0, 1, 3, 2).reshape(g * 512, n)


E2M1 = np.array([0.0, 0.5, 1.0, 1.5, 2.0, 3.0, 4.0, 6.0, -0.0, -0.5, -1.0, -1.5, -2.0, -3.0, -4.0, -6.0])


def pack_fp4(w):
    k, n = w.shape
    w = f64(np.asarray(w, np.float32).astype(ml_dtypes.bfloat16)).reshape(k // 32, 32, n)
    amax = np.abs(w).max(1)
    mant, ex = np.frexp(amax / 6.0)
    byte = np.clip(np.where(amax > 0, np.where(mant > 0.5, ex, ex - 1) + 127, 1), 1, 254)
    scaled = (w * np.exp2(127.0 - byte)[:, None, :]).reshape(k, n).astype(np.float32)
    c = np.ascontiguousarray(scaled.reshape(k // 512, 128, 4, n).transpose(0, 1, 3, 2)).astype(ml_dtypes.float4_e2m1fn).view(np.uint8) & 0xF
    words = (c[..., 0::2] | (c[..., 1::2] << 4)).reshape(k // 512, 128, 2 * n)
    return np.ascontiguousarray(words), np.ascontiguousarray(byte.astype(np.uint8).reshape(k // 512, 16, n))


def unpack_fp4(words, scales):
    g, _, n = scales.shape
    words = np.ascontiguousarray(words).reshape(g, 128, n, 2)
    nib = np.empty((g, 128, n, 4), np.uint8)
    nib[..., 0::2] = words & 0xF
    nib[..., 1::2] = words >> 4
    vals = E2M1[nib] * np.repeat(np.exp2(scales.astype(np.float64) - 127.0), 8, axis=1)[..., None]
    return vals.transpose(0, 1, 3, 2).reshape(g * 512, n)


def sigmoid(v):
    return 1.0 / (1.0 + np.exp(-np.maximum(v, -700.0)))

def planes(y):
    n, m = y.shape
    v = y.astype(np.float32).astype(ml_dtypes.bfloat16).astype(np.float64).reshape(n // 32, 32, m)
    top = np.abs(v).max(1)
    byte = np.clip(np.where(top > 0, np.frexp(top)[1] - 1 + 127 - 7, 1), 1, 254)
    codes = (v * np.exp2(127.0 - byte)[:, None, :]).reshape(n, m).astype(np.float32).astype(ml_dtypes.float8_e4m3fn).view(np.uint8)
    words = codes.reshape(n // 512, 128, 4, m).transpose(0, 1, 3, 2)
    return np.ascontiguousarray(words), np.ascontiguousarray(byte.astype(np.uint8).reshape(n // 512, 16, m))


K, T, S, N, H, W = 512, 2048, 512, 512, 512, 256


def setup_inputs():
    n = np.random.standard_normal
    s = mx_kscale(K)[:, None]
    u = mx_kscale(H)
    packed_xT = pack_weight(n((K, T)) * s)
    packed_w1 = pack_fp4(n((K, H)) / np.sqrt(K) / s)
    packed_w2 = pack_fp4(n((H, N)) / np.sqrt(2 * H) / u[:, None])
    packed_w3 = pack_fp4(n((H, N)) / np.sqrt(2 * H) / u[:, None])
    perm = np.stack([np.random.permutation(S) for _ in range(8)])
    return {
        "x_words": packed_xT[0],
        "x_scales": packed_xT[1],
        "w1_words": packed_w1[0],
        "w1_scales": packed_w1[1],
        "gn": (np.random.uniform(0.5, 1.5, (H, 1)) * u[:, None]).astype(np.float32),
        "gm": (np.random.uniform(0.5, 1.5, (H, 1)) * u[:, None]).astype(np.float32),
        "w2_words": packed_w2[0],
        "w2_scales": packed_w2[1],
        "w3_words": packed_w3[0],
        "w3_scales": packed_w3[1],
        "offs": striped(np.random.permutation(T)[:S]),
        "n1": striped8(perm[:, :W]),
        "n2": striped8(perm[:, W:]),
        "n3": striped8(np.stack([np.random.permutation(S) for _ in range(8)])),
        "n4": striped8(np.stack([np.random.permutation(S) for _ in range(8)])),
        "n5": striped8(np.stack([np.random.permutation(S) for _ in range(8)])),
        "n6": striped8(np.stack([np.random.permutation(S) for _ in range(8)])),
    }


def reference(x_words, x_scales, w1_words, w1_scales, gn, gm, w2_words, w2_scales, w3_words, w3_scales, offs, n1, n2, n3, n4, n5, n6):
    xq = unpack_weight(x_words, x_scales)[:, unstriped(offs)]
    y = unpack_fp4(w1_words, w1_scales).T @ xq
    pa = y[np.arange(H)[:, None], runs(n1, H)]
    pb = y[np.arange(H)[:, None], runs(n2, H)]
    rb = np.maximum(0.5 * pa, pb)
    ra = pb - pa
    ds = np.zeros((H, S))
    ds[np.arange(H)[:, None], runs(n1, H)] = ra
    dt = ds.copy()
    dt[np.arange(H)[:, None], runs(n2, H)] = rb
    z = f64(gn) * dt
    st = y * (sigmoid(y[np.arange(H)[:, None], runs(n3, H)]))
    z2 = f64(gm) * (st - (st[np.arange(H)[:, None], runs(n4, H)]))
    h = unpack_fp4(w2_words, w2_scales).T @ mxq(z, 0, "e4m3") + unpack_fp4(w3_words, w3_scales).T @ mxq(z2, 0, "e4m3")
    pa2 = h[np.arange(N)[:, None], runs(n5, N)]
    kr = np.exp(-0.5 * ((h - pa2) ** 2))
    pb2 = h[np.arange(N)[:, None], runs(n6, N)]
    kr2 = np.exp(-0.5 * ((h - pb2) ** 2))
    out_0 = (kr * pa2 + kr2 * pb2) / (kr + kr2 + 0.5)
    return (out_0,) + planes(out_0)

@@ -1,0 +1,340 @@
+from contextlib import ExitStack
+
+import concourse.mybir as mybir
+
+F32 = mybir.dt.float32
+BF16 = mybir.dt.bfloat16
+I32 = mybir.dt.int32
+U32 = mybir.dt.uint32
+U16 = mybir.dt.uint16
+U8 = mybir.dt.uint8
+FP8X4 = mybir.dt.float8_e4m3fn_x4
+FP4X4 = mybir.dt.float4_e2m1fn_x4
+ACT = mybir.ActivationFunctionType
+ALU = mybir.AluOpType
+
+P = 128
+PACK = 4
+T = 2048
+S = 512
+HALF = S // 2
+FLOPS = 3 * 2 * 512 * 512 * 512
+
+
+def tile_picked_joinlifthopgkern_none_po_kernel(
+    tc, x_words, x_scales, w1_words, w1_scales, gn, gm, w2_words, w2_scales, w3_words, w3_scales,
+    offs, n1, n2, n3, n4, n5, n6, out_0, out_1, out_2,
+):
+    nc = tc.nc
+    halves = [slice(0, HALF), slice(HALF, S)]
+    list_halves = [slice(0, HALF // 16), slice(HALF // 16, S // 16)]
+
+    with ExitStack() as ctx:
+        keep = ctx.enter_context(tc.tile_pool(name="keep", bufs=1))
+        psum = ctx.enter_context(tc.psum_pool(name="psum", bufs=1))
+
+        def sb(name, shape, dtype, tag=None):
+            return keep.tile(shape, dtype, name=name, tag=tag or name, align_bytes=64)
+
+        def load_list(name, src):
+            tile = sb(name, list(src.shape), U16)
+            nc.sync.dma_start(tile[:], src)
+            return tile
+
+        def load_scale_rows(queue, tile_cols, src, q):
+            queue.dma_start(tile_cols[32 * q : 32 * q + 4, :].bitcast(I32), src[0, 4 * q : 4 * q + 4, :].bitcast(I32))
+
+        def deal_words(name, raw, tag=None):
+            dealt = sb(name, [P, 2 * S], U8, tag)
+            nc.scalar.copy(
+                out=dealt[:].bitcast(U16).rearrange("p (t m) -> p t m", t=PACK),
+                in_=raw[:].bitcast(U16).rearrange("p (m t) -> p t m", t=PACK),
+            )
+            return dealt
+
+        def deal_scales(name, raw, tag=None):
+            dealt = sb(name, [P, S], U8, tag)
+            nc.vector.tensor_copy(
+                out=dealt[:].rearrange("p (t m) -> p t m", t=PACK),
+                in_=raw[:].rearrange("p (m t) -> p t m", t=PACK),
+            )
+            return dealt
+
+        def product(out, words, scales, t, codes, code_scales, cols, start, stop):
+            nc.tensor.matmul_mx(
+                out=out,
+                lhsT=words[:, 2 * P * t : 2 * P * (t + 1)].bitcast(FP4X4),
+                lhsT_scale=scales[:, P * t : P * (t + 1)],
+                rhs=codes[:, cols].bitcast(FP8X4),
+                rhs_scale=code_scales[:, cols],
+                start=start,
+                stop=stop,
+            )
+
+        def gather(engine, out, window, offsets):
+            if engine is nc.vector:
+                nc.vector.tensor_copy(out, window[:].indirect(offsets))
+            else:
+                nc.scalar.activation(out, window[:].indirect(offsets), ACT.Copy)
+
+        def weave(engine, woven, planes, cols):
+            dst = woven[:, cols, :].rearrange("p (c i) t -> p c t i", i=4)
+            src = planes[:, :, cols].rearrange("p t (c i) -> p c t i", i=4)
+            if engine is nc.vector:
+                nc.vector.tensor_copy(out=dst, in_=src)
+            else:
+                nc.scalar.copy(out=dst, in_=src)
+
+        def quantise(codes, scales, woven, cols):
+            nc.vector.quantize_mx(
+                out=codes[:, cols].bitcast(FP8X4),
+                scales=scales[:, cols],
+                in_=woven[:, cols, :].rearrange("p c t -> p (c t)"),
+            )
+
+        w1s_raw = sb("w1s_raw", [P, S], U8)
+        xs_all = sb("xs_all", [P, T], U8)
+        w2s_raw = sb("w2s_raw", [P, S], U8)
+        w3s_raw = sb("w3s_raw", [P, S], U8)
+        nc.gpsimd.memset(w1s_raw[:].bitcast(I32), 0)
+        for tile in (xs_all, w3s_raw, w2s_raw):
+            nc.vector.memset(tile[:].bitcast(I32), 0)
+
+        offs_sb = load_list("offs_sb", offs)
+        w1w_raw = sb("w1w_raw", [P, 2 * S], U8)
+        nc.sync.dma_start(w1w_raw[:].bitcast(I32), w1_words[0].bitcast(I32))
+        xw_all = sb("xw_all", [P, T], U32)
+        nc.sync.dma_start(xw_all[:].bitcast(I32), x_words[0].rearrange("p n t -> p (n t)").bitcast(I32))
+        load_scale_rows(nc.gpsimd, w1s_raw, w1_scales, 1)
+        load_scale_rows(nc.gpsimd, w1s_raw, w1_scales, 2)
+        for q in range(4):
+            load_scale_rows(nc.sync, xs_all, x_scales, q)
+        load_scale_rows(nc.sync, w1s_raw, w1_scales, 0)
+        load_scale_rows(nc.sync, w1s_raw, w1_scales, 3)
+        w3w_raw = sb("w3w_raw", [P, 2 * S], U8)
+        nc.sync.dma_start(w3w_raw[:].bitcast(I32), w3_words[0].bitcast(I32))
+        n1_sb = load_list("n1_sb", n1)
+        n2_sb = load_list("n2_sb", n2)
+        n3_sb = load_list("n3_sb", n3)
+        gm_sb = sb("gm_sb", [P, PACK], F32)
+        nc.sync.dma_start(gm_sb[:], gm.rearrange("(p t) o -> p (t o)", t=PACK))
+        n4_sb = load_list("n4_sb", n4)
+        for q in range(4):
+            load_scale_rows(nc.sync, w3s_raw, w3_scales, q)
+        gn_sb = sb("gn_sb", [P, PACK], F32)
+        nc.sync.dma_start(gn_sb[:], gn.rearrange("(p t) o -> p (t o)", t=PACK))
+        w2w_raw = sb("w2w_raw", [P, 2 * S], U8)
+        nc.sync.dma_start(w2w_raw[:].bitcast(I32), w2_words[0].bitcast(I32))
+        for q in range(4):
+            load_scale_rows(nc.sync, w2s_raw, w2_scales, q)
+        n5_sb = load_list("n5_sb", n5)
+        n6_sb = load_list("n6_sb", n6)
+
+        w1w = deal_words("w1w", w1w_raw)
+        w3w = deal_words("w3w", w3w_raw)
+        xs = sb("xs", [P, S], U8)
+        nc.vector.tensor_copy(xs[:], xs_all[:].indirect(offs_sb[:]))
+        w1s = deal_scales("w1s", w1s_raw)
+        xw = sb("xw", [P, S], U32)
+        for cols, lcols in zip(halves, list_halves):
+            nc.vector.tensor_copy(xw[:, cols], xw_all[:].indirect(offs_sb[:, lcols]))
+
+        y_first = [psum.tile([P, HALF], F32, name="y_first%d" % u, tag="bank%d" % u) for u in range(2)]
+        y_banks = [None] + [psum.tile([P, S], F32, name="y_bank%d" % t, tag="bank%d" % (t + 1)) for t in range(1, PACK)]
+        for u in range(2):
+            product(y_first[u][:], w1w, w1s, 0, xw, xs, halves[u], True, True)
+        for t in range(1, PACK):
+            product(y_banks[t][:], w1w, w1s, t, xw, xs, slice(0, S), True, True)
+
+        z_planes = sb("z_planes", [P, PACK, S], BF16)
+        z2_planes = sb("z2_planes", [P, PACK, S], BF16)
+        last = PACK - 1
+        y = [sb("y%d" % t, [P, S], F32) for t in range(PACK)]
+        neg_pa = [sb("neg_pa%d" % t, [P, HALF], F32) for t in range(PACK)]
+        pb = [sb("pb%d" % t, [P, HALF], F32) for t in range(PACK)]
+        gate = [sb("gate%d" % t, [P, S], F32) for t in range(PACK)]
+        st = [sb("st%d" % t, [P, S], F32) for t in range(PACK)]
+        hop = [sb("hop%d" % t, [P, S], F32) for t in range(PACK)]
+        dt = {}
+
+        def fetch_pairs(t):
+            nc.scalar.activation(neg_pa[t][:], y[t][:].indirect(n1_sb[:]), ACT.Copy, scale=-1.0)
+            gather(nc.scalar, pb[t][:], y[t], n2_sb[:])
+
+        def put_ra(t, tag=None):
+            dt[t] = sb("dt%d" % t, [P, S], F32, tag)
+            nc.vector.tensor_tensor(dt[t][:].indirect(n1_sb[:]), pb[t][:], neg_pa[t][:], ALU.add)
+
+        def make_rb(t, tag=None):
+            rb = sb("rb%d" % t, [P, HALF], F32, tag)
+            nc.vector.scalar_tensor_tensor(rb[:], neg_pa[t][:], -0.5, pb[t][:], ALU.mult, ALU.max)
+            return rb
+
+        def put_rb(t, rb):
+            nc.vector.tensor_copy(dt[t][:].indirect(n2_sb[:]), rb[:])
+
+        def make_st(t):
+            nc.vector.scalar_tensor_tensor(st[t][:], y[t][:], gm_sb[:, t : t + 1], gate[t][:], ALU.mult, ALU.mult)
+
+        def fetch_gate(t):
+            for cols, lcols in zip(halves, list_halves):
+                nc.scalar.activation(gate[t][:, cols], y[t][:].indirect(n3_sb[:, lcols]), ACT.Sigmoid)
+            make_st(t)
+
+        def fetch_hop(t):
+            for cols, lcols in zip(halves, list_halves):
+                gather(nc.scalar, hop[t][:, cols], st[t], n4_sb[:, lcols])
+            nc.vector.tensor_tensor(z2_planes[:, t, :], st[t][:], hop[t][:], ALU.subtract)
+
+        def gain(t):
+            nc.scalar.activation(z_planes[:, t, :], dt[t][:], ACT.Copy, scale=gn_sb[:, t : t + 1])
+
+        sig0 = sb("sig0", [P, S], F32)
+        nc.scalar.activation(sig0[:, halves[0]], y_first[0][:], ACT.Sigmoid)
+        nc.scalar.copy(out=y[0][:, halves[0]], in_=y_first[0][:])
+        nc.vector.tensor_copy(out=y[0][:, halves[1]], in_=y_first[1][:])
+        nc.vector.tensor_scalar(neg_pa[0][:], y[0][:].indirect(n1_sb[:]), -1.0, 0.0, ALU.mult, ALU.add)
+        gather(nc.scalar, pb[0][:], y[0], n2_sb[:])
+        rb = make_rb(0)
+        put_ra(0)
+        w3s = deal_scales("w3s", w3s_raw, "neg_pa0")
+        put_rb(0, rb)
+        nc.scalar.activation(sig0[:, halves[1]], y_first[1][:], ACT.Sigmoid)
+        nc.scalar.copy(out=y[1][:], in_=y_banks[1][:])
+        for cols, lcols in zip(halves, list_halves):
+            gather(nc.scalar, gate[0][:, cols], sig0, n3_sb[:, lcols])
+        make_st(0)
+        fetch_pairs(1)
+        rb = make_rb(1)
+        put_ra(1)
+        w2s = deal_scales("w2s", w2s_raw, "neg_pa1")
+        put_rb(1, rb)
+        nc.scalar.copy(out=y[2][:], in_=y_banks[2][:])
+        fetch_gate(1)
+        fetch_hop(0)
+        fetch_gate(2)
+        nc.scalar.copy(out=y[3][:], in_=y_banks[3][:])
+        fetch_pairs(2)
+        put_ra(2)
+        fetch_hop(1)
+        fetch_gate(3)
+        put_rb(2, make_rb(2, "gate3"))
+        gain(0)
+        fetch_hop(2)
+        fetch_pairs(3)
+        fetch_hop(3)
+        put_ra(3, "hop3")
+        gain(1)
+
+        z2_woven = sb("z2_woven", [P, S, PACK], BF16)
+        z2_codes = sb("z2_codes", [P, S], U32)
+        z2_scales = sb("z2_scales", [P, S], U8)
+        z_woven = sb("z_woven", [P, S, PACK], BF16)
+        z_codes = sb("z_codes", [P, S], U32)
+        z_scales = sb("z_scales", [P, S], U8)
+        for cols in halves:
+            weave(nc.scalar, z2_woven, z2_planes, cols)
+        for cols in halves:
+            quantise(z2_codes, z2_scales, z2_woven, cols)
+        put_rb(3, make_rb(3, "z2_woven"))
+        w2w = deal_words("w2w", w2w_raw, "z2_planes")
+        gain(2)
+        nc.vector.tensor_scalar(z_planes[:, last, :], dt[last][:], gn_sb[:, last : last + 1], None, ALU.mult)
+        weave(nc.vector, z_woven, z_planes, slice(0, HALF))
+        weave(nc.scalar, z_woven, z_planes, slice(3 * S // 4, S))
+        weave(nc.vector, z_woven, z_planes, slice(HALF, 3 * S // 4))
+        for cols in halves:
+            quantise(z_codes, z_scales, z_woven, cols)
+
+        h_first = [psum.tile([P, HALF], F32, name="h_first%d" % u, tag="bank%d" % (5 + u)) for u in range(2)]
+        h_tags = [None, "bank7", "bank0", "bank1"]
+        h_banks = [None] + [psum.tile([P, S], F32, name="h_bank%d" % t, tag=h_tags[t]) for t in range(1, PACK)]
+        groups = [(h_first[u][:], 0, halves[u]) for u in range(2)]
+        groups.extend((h_banks[t][:], t, slice(0, S)) for t in range(1, PACK))
+        for bank, t, cols in groups:
+            product(bank, w3w, w3s, t, z2_codes, z2_scales, cols, True, False)
+        for bank, t, cols in groups:
+            product(bank, w2w, w2s, t, z_codes, z_scales, cols, False, True)
+
+        num = sb("num", [P, PACK, S], F32)
+        ksum = sb("ksum", [P, PACK, S], F32)
+        den_sq = sb("den_sq", [P, PACK, S], F32)
+        h = [sb("h%d" % t, [P, S], F32) for t in range(PACK)]
+        near = [sb("near%d" % t, [P, 2, S], F32) for t in range(PACK)]
+        diff = [sb("diff%d" % t, [P, 2, S], F32) for t in range(PACK)]
+        sq = [sb("sq%d" % t, [P, 2, S], F32) for t in range(PACK)]
+        kern = [sb("kern%d" % t, [P, 2, S], F32) for t in range(PACK)]
+        near_lists = [n5_sb, n6_sb]
+
+        def fetch_near(engine, t, b):
+            for cols, lcols in zip(halves, list_halves):
+                gather(engine, near[t][:, b, cols], h[t], near_lists[b][:, lcols])
+
+        def differences(t):
+            both = h[t][:].unsqueeze(1).to_broadcast([P, 2, S])
+            nc.vector.tensor_tensor(diff[t][:], near[t][:], both, ALU.subtract)
+
+        def kernels(t):
+            nc.scalar.activation(sq[t][:], diff[t][:], ACT.Square)
+            nc.scalar.activation(kern[t][:], sq[t][:], ACT.Exp, scale=-0.5)
+
+        def sums(t):
+            weighted = sb("weighted%d" % t, [P, 2, S], F32)
+            nc.vector.tensor_tensor(weighted[:], kern[t][:], near[t][:], ALU.mult)
+            nc.vector.tensor_tensor(ksum[:, t, :], kern[t][:, 0, :], kern[t][:, 1, :], ALU.add)
+            nc.vector.tensor_tensor(num[:, t, :], weighted[:, 0, :], weighted[:, 1, :], ALU.add)
+
+        def square_den(t):
+            nc.scalar.activation(den_sq[:, t, :], ksum[:, t, :], ACT.Square, bias=0.5)
+
+        nc.scalar.copy(out=h[0][:, halves[0]], in_=h_first[0][:])
+        nc.vector.tensor_copy(out=h[0][:, halves[1]], in_=h_first[1][:])
+        fetch_near(nc.vector, 0, 0)
+        fetch_near(nc.scalar, 0, 1)
+        nc.scalar.copy(out=h[1][:], in_=h_banks[1][:])
+        differences(0)
+        fetch_near(nc.vector, 1, 0)
+        fetch_near(nc.scalar, 1, 1)
+        nc.vector.tensor_copy(out=h[2][:], in_=h_banks[2][:])
+        differences(1)
+        kernels(0)
+        fetch_near(nc.vector, 2, 0)
+        fetch_near(nc.vector, 2, 1)
+        differences(2)
+        kernels(1)
+        sums(0)
+        nc.scalar.copy(out=h[3][:], in_=h_banks[3][:])
+        fetch_near(nc.scalar, 3, 1)
+        fetch_near(nc.vector, 3, 0)
+        differences(3)
+        kernels(2)
+        sums(1)
+        kernels(3)
+        sums(2)
+        square_den(0)
+        square_den(1)
+        sums(3)
+
+        recip = sb("recip", [P, PACK, S], F32, "sq%d" % last)
+        res = sb("res", [P, PACK, S], F32)
+        out_rows = out_0.rearrange("(p t) c -> p t c", t=PACK)
+        for t in range(PACK):
+            if t >= 2:
+                square_den(t)
+            nc.scalar.activation(recip[:, t, :], den_sq[:, t, :], ACT.Abs_reciprocal_sqrt)
+            nc.vector.tensor_tensor(res[:, t, :], num[:, t, :], recip[:, t, :], ALU.mult)
+            nc.sync.dma_start(out_rows[:, t, :], res[:, t, :])
+
+        o_woven = sb("o_woven", [P, S, PACK], BF16)
+        o_codes = sb("o_codes", [P, S], U32)
+        o_scales = sb("o_scales", [P, S], U8)
+        weave(nc.vector, o_woven, res, halves[0])
+        weave(nc.scalar, o_woven, res, slice(3 * S // 4, S))
+        weave(nc.vector, o_woven, res, slice(HALF, 3 * S // 4))
+        out_words = out_1[0].rearrange("p n t -> p (n t)").bitcast(I32)
+        for cols in halves:
+            quantise(o_codes, o_scales, o_woven, cols)
+            nc.sync.dma_start(out_words[:, cols], o_codes[:, cols].bitcast(I32))
+        for q in range(4):
+            queue = nc.sync if q % 2 == 0 else nc.scalar
+            queue.dma_start(out_2[0, 4 * q : 4 * q + 4, :].bitcast(I32), o_scales[32 * q : 32 * q + 4, :].bitcast(I32))

@@ -42,7 +42,8 @@ def tile_picked_joinlifthopgkern_none_po_kernel(
             return tile
 
         def load_scale_rows(queue, tile_cols, src, q):
-            queue.dma_start(tile_cols[32 * q : 32 * q + 4, :].bitcast(I32), src[0, 4 * q : 4 * q + 4, :].bitcast(I32))
+            rows = src[0, 4 * q : 4 * q + 4, :].bitcast(I32).partition_broadcast(8)
+            queue.dma_start(tile_cols[32 * q : 32 * q + 32, :].bitcast(I32), rows)
 
         def deal_words(name, raw, tag=None):
             dealt = sb(name, [P, 2 * S], U8, tag)
@@ -96,23 +97,18 @@ def tile_picked_joinlifthopgkern_none_po_kernel(
         xs_all = sb("xs_all", [P, T], U8)
         w2s_raw = sb("w2s_raw", [P, S], U8)
         w3s_raw = sb("w3s_raw", [P, S], U8)
-        nc.gpsimd.memset(w1s_raw[:].bitcast(I32), 0)
-        for tile in (xs_all, w3s_raw, w2s_raw):
-            nc.vector.memset(tile[:].bitcast(I32), 0)
 
         offs_sb = load_list("offs_sb", offs)
+        for q in range(4):
+            load_scale_rows(nc.sync if q < 2 else nc.scalar, xs_all, x_scales, q)
         w1w_raw = sb("w1w_raw", [P, 2 * S], U8)
-        nc.sync.dma_start(w1w_raw[:].bitcast(I32), w1_words[0].bitcast(I32))
+        nc.scalar.dma_start(w1w_raw[:].bitcast(I32), w1_words[0].bitcast(I32))
         xw_all = sb("xw_all", [P, T], U32)
         nc.sync.dma_start(xw_all[:].bitcast(I32), x_words[0].rearrange("p n t -> p (n t)").bitcast(I32))
-        load_scale_rows(nc.gpsimd, w1s_raw, w1_scales, 1)
+        load_scale_rows(nc.scalar, w1s_raw, w1_scales, 0)
+        load_scale_rows(nc.scalar, w1s_raw, w1_scales, 1)
         load_scale_rows(nc.gpsimd, w1s_raw, w1_scales, 2)
-        for q in range(4):
-            load_scale_rows(nc.sync, xs_all, x_scales, q)
-        load_scale_rows(nc.sync, w1s_raw, w1_scales, 0)
-        load_scale_rows(nc.sync, w1s_raw, w1_scales, 3)
-        w3w_raw = sb("w3w_raw", [P, 2 * S], U8)
-        nc.sync.dma_start(w3w_raw[:].bitcast(I32), w3_words[0].bitcast(I32))
+        load_scale_rows(nc.gpsimd, w1s_raw, w1_scales, 3)
         n1_sb = load_list("n1_sb", n1)
         n2_sb = load_list("n2_sb", n2)
         n3_sb = load_list("n3_sb", n3)
@@ -121,6 +117,8 @@ def tile_picked_joinlifthopgkern_none_po_kernel(
         n4_sb = load_list("n4_sb", n4)
         for q in range(4):
             load_scale_rows(nc.sync, w3s_raw, w3_scales, q)
+        w3w_raw = sb("w3w_raw", [P, 2 * S], U8)
+        nc.sync.dma_start(w3w_raw[:].bitcast(I32), w3_words[0].bitcast(I32))
         gn_sb = sb("gn_sb", [P, PACK], F32)
         nc.sync.dma_start(gn_sb[:], gn.rearrange("(p t) o -> p (t o)", t=PACK))
         w2w_raw = sb("w2w_raw", [P, 2 * S], U8)
@@ -131,11 +129,10 @@ def tile_picked_joinlifthopgkern_none_po_kernel(
         n6_sb = load_list("n6_sb", n6)
 
         w1w = deal_words("w1w", w1w_raw)
-        w3w = deal_words("w3w", w3w_raw)
         xs = sb("xs", [P, S], U8)
         nc.vector.tensor_copy(xs[:], xs_all[:].indirect(offs_sb[:]))
         w1s = deal_scales("w1s", w1s_raw)
-        xw = sb("xw", [P, S], U32)
+        xw = sb("xw", [P, S], U32, "xs_all")
         for cols, lcols in zip(halves, list_halves):
             nc.vector.tensor_copy(xw[:, cols], xw_all[:].indirect(offs_sb[:, lcols]))
 
@@ -146,85 +143,90 @@ def tile_picked_joinlifthopgkern_none_po_kernel(
         for t in range(1, PACK):
             product(y_banks[t][:], w1w, w1s, t, xw, xs, slice(0, S), True, True)
 
-        z_planes = sb("z_planes", [P, PACK, S], BF16)
-        z2_planes = sb("z2_planes", [P, PACK, S], BF16)
+        z_planes = sb("z_planes", [P, PACK * S], BF16)
+        z2_planes = sb("z2_planes", [P, PACK * S], BF16)
         last = PACK - 1
+
+        def plane(planes, t):
+            return planes[:, S * t : S * (t + 1)]
+
         y = [sb("y%d" % t, [P, S], F32) for t in range(PACK)]
-        neg_pa = [sb("neg_pa%d" % t, [P, HALF], F32) for t in range(PACK)]
-        pb = [sb("pb%d" % t, [P, HALF], F32) for t in range(PACK)]
         gate = [sb("gate%d" % t, [P, S], F32) for t in range(PACK)]
-        st = [sb("st%d" % t, [P, S], F32) for t in range(PACK)]
         hop = [sb("hop%d" % t, [P, S], F32) for t in range(PACK)]
+        st = [sb("st%d" % t, [P, S], F32) for t in range(PACK)]
+        rb = [sb("rb%d" % t, [P, HALF], F32) for t in range(PACK)]
+        neg_pa0 = sb("neg_pa0", [P, HALF], F32)
+        pb0 = sb("pb0", [P, HALF], F32)
+        neg_pa = [neg_pa0[:], plane(z_planes, 0).bitcast(F32), plane(z2_planes, 2).bitcast(F32), plane(z_planes, 1).bitcast(F32)]
+        pb = [pb0[:], plane(z2_planes, 0).bitcast(F32), plane(z2_planes, 1).bitcast(F32), plane(z2_planes, 3).bitcast(F32)]
         dt = {}
 
-        def fetch_pairs(t):
-            nc.scalar.activation(neg_pa[t][:], y[t][:].indirect(n1_sb[:]), ACT.Copy, scale=-1.0)
-            gather(nc.scalar, pb[t][:], y[t], n2_sb[:])
-
-        def put_ra(t, tag=None):
+        def put_pairs(t, tag=None):
+            nc.vector.scalar_tensor_tensor(rb[t][:], neg_pa[t], -0.5, pb[t], ALU.mult, ALU.max)
             dt[t] = sb("dt%d" % t, [P, S], F32, tag)
-            nc.vector.tensor_tensor(dt[t][:].indirect(n1_sb[:]), pb[t][:], neg_pa[t][:], ALU.add)
+            nc.vector.tensor_tensor(dt[t][:].indirect(n1_sb[:]), pb[t], neg_pa[t], ALU.add)
 
-        def make_rb(t, tag=None):
-            rb = sb("rb%d" % t, [P, HALF], F32, tag)
-            nc.vector.scalar_tensor_tensor(rb[:], neg_pa[t][:], -0.5, pb[t][:], ALU.mult, ALU.max)
-            return rb
+        def put_rb(t):
+            nc.vector.tensor_copy(dt[t][:].indirect(n2_sb[:]), rb[t][:])
 
-        def put_rb(t, rb):
-            nc.vector.tensor_copy(dt[t][:].indirect(n2_sb[:]), rb[:])
+        def fetch_pairs(t, tag=None):
+            nc.scalar.activation(neg_pa[t], y[t][:].indirect(n1_sb[:]), ACT.Copy, scale=-1.0)
+            gather(nc.scalar, pb[t], y[t], n2_sb[:])
+            put_pairs(t, tag)
+            put_rb(t)
 
-        def make_st(t):
-            nc.vector.scalar_tensor_tensor(st[t][:], y[t][:], gm_sb[:, t : t + 1], gate[t][:], ALU.mult, ALU.mult)
+        def make_st(cols, t, bank):
+            nc.vector.scalar_tensor_tensor(st[t][:, cols], bank, gm_sb[:, t : t + 1], gate[t][:, cols], ALU.mult, ALU.mult)
 
         def fetch_gate(t):
             for cols, lcols in zip(halves, list_halves):
                 nc.scalar.activation(gate[t][:, cols], y[t][:].indirect(n3_sb[:, lcols]), ACT.Sigmoid)
-            make_st(t)
+            make_st(slice(0, S), t, y_banks[t][:])
 
         def fetch_hop(t):
             for cols, lcols in zip(halves, list_halves):
                 gather(nc.scalar, hop[t][:, cols], st[t], n4_sb[:, lcols])
-            nc.vector.tensor_tensor(z2_planes[:, t, :], st[t][:], hop[t][:], ALU.subtract)
+            nc.gpsimd.tensor_tensor(plane(z2_planes, t), st[t][:], hop[t][:], ALU.subtract)
 
-        def gain(t):
-            nc.scalar.activation(z_planes[:, t, :], dt[t][:], ACT.Copy, scale=gn_sb[:, t : t + 1])
+        def gain(t, engine):
+            if engine is nc.scalar:
+                nc.scalar.activation(plane(z_planes, t), dt[t][:], ACT.Copy, scale=gn_sb[:, t : t + 1])
+            else:
+                engine.tensor_scalar(plane(z_planes, t), dt[t][:], gn_sb[:, t : t + 1], 0.0, ALU.mult, ALU.add)
 
         sig0 = sb("sig0", [P, S], F32)
         nc.scalar.activation(sig0[:, halves[0]], y_first[0][:], ACT.Sigmoid)
         nc.scalar.copy(out=y[0][:, halves[0]], in_=y_first[0][:])
         nc.vector.tensor_copy(out=y[0][:, halves[1]], in_=y_first[1][:])
-        nc.vector.tensor_scalar(neg_pa[0][:], y[0][:].indirect(n1_sb[:]), -1.0, 0.0, ALU.mult, ALU.add)
-        gather(nc.scalar, pb[0][:], y[0], n2_sb[:])
-        rb = make_rb(0)
-        put_ra(0)
+        nc.vector.tensor_scalar(neg_pa[0], y[0][:].indirect(n1_sb[:]), -1.0, 0.0, ALU.mult, ALU.add)
+        gather(nc.scalar, pb[0], y[0], n2_sb[:])
+        put_pairs(0)
         w3s = deal_scales("w3s", w3s_raw, "neg_pa0")
-        put_rb(0, rb)
+        w2s = deal_scales("w2s", w2s_raw, "pb0")
+        put_rb(0)
         nc.scalar.activation(sig0[:, halves[1]], y_first[1][:], ACT.Sigmoid)
         nc.scalar.copy(out=y[1][:], in_=y_banks[1][:])
         for cols, lcols in zip(halves, list_halves):
             gather(nc.scalar, gate[0][:, cols], sig0, n3_sb[:, lcols])
-        make_st(0)
+        for u in range(2):
+            make_st(halves[u], 0, y_first[u][:])
         fetch_pairs(1)
-        rb = make_rb(1)
-        put_ra(1)
-        w2s = deal_scales("w2s", w2s_raw, "neg_pa1")
-        put_rb(1, rb)
         nc.scalar.copy(out=y[2][:], in_=y_banks[2][:])
         fetch_gate(1)
         fetch_hop(0)
+        gain(0, nc.gpsimd)
         fetch_gate(2)
+        fetch_pairs(2, "gate2")
         nc.scalar.copy(out=y[3][:], in_=y_banks[3][:])
-        fetch_pairs(2)
-        put_ra(2)
         fetch_hop(1)
-        fetch_gate(3)
-        put_rb(2, make_rb(2, "gate3"))
-        gain(0)
         fetch_hop(2)
-        fetch_pairs(3)
+        fetch_gate(3)
+        fetch_pairs(3, "gate3")
         fetch_hop(3)
-        put_ra(3, "hop3")
-        gain(1)
+        w3w = deal_words("w3w", w3w_raw, "hop1")
+        w2w = deal_words("w2w", w2w_raw, "hop2")
+        gain(1, nc.scalar)
+        gain(2, nc.scalar)
 
         z2_woven = sb("z2_woven", [P, S, PACK], BF16)
         z2_codes = sb("z2_codes", [P, S], U32)
@@ -232,33 +234,30 @@ def tile_picked_joinlifthopgkern_none_po_kernel(
         z_woven = sb("z_woven", [P, S, PACK], BF16)
         z_codes = sb("z_codes", [P, S], U32)
         z_scales = sb("z_scales", [P, S], U8)
+        gain(last, nc.vector)
         for cols in halves:
-            weave(nc.scalar, z2_woven, z2_planes, cols)
-        for cols in halves:
-            quantise(z2_codes, z2_scales, z2_woven, cols)
-        put_rb(3, make_rb(3, "z2_woven"))
-        w2w = deal_words("w2w", w2w_raw, "z2_planes")
-        gain(2)
-        nc.vector.tensor_scalar(z_planes[:, last, :], dt[last][:], gn_sb[:, last : last + 1], None, ALU.mult)
-        weave(nc.vector, z_woven, z_planes, slice(0, HALF))
-        weave(nc.scalar, z_woven, z_planes, slice(3 * S // 4, S))
-        weave(nc.vector, z_woven, z_planes, slice(HALF, 3 * S // 4))
+            weave(nc.scalar, z2_woven, z2_planes[:].rearrange("p (t c) -> p t c", t=PACK), cols)
+        weave(nc.vector, z_woven, z_planes[:].rearrange("p (t c) -> p t c", t=PACK), slice(0, HALF))
+        weave(nc.vector, z_woven, z_planes[:].rearrange("p (t c) -> p t c", t=PACK), slice(HALF, S))
         for cols in halves:
             quantise(z_codes, z_scales, z_woven, cols)
+            quantise(z2_codes, z2_scales, z2_woven, cols)
 
         h_first = [psum.tile([P, HALF], F32, name="h_first%d" % u, tag="bank%d" % (5 + u)) for u in range(2)]
-        h_tags = [None, "bank7", "bank0", "bank1"]
+        h_tags = [None, "bank5", "bank6", "bank6"]
         h_banks = [None] + [psum.tile([P, S], F32, name="h_bank%d" % t, tag=h_tags[t]) for t in range(1, PACK)]
         groups = [(h_first[u][:], 0, halves[u]) for u in range(2)]
         groups.extend((h_banks[t][:], t, slice(0, S)) for t in range(1, PACK))
         for bank, t, cols in groups:
-            product(bank, w3w, w3s, t, z2_codes, z2_scales, cols, True, False)
-        for bank, t, cols in groups:
-            product(bank, w2w, w2s, t, z_codes, z_scales, cols, False, True)
+            passes = [(w3w, w3s, t, z2_codes, z2_scales), (w2w, w2s, t, z_codes, z_scales)]
+            if t == 0:
+                passes = passes[::-1]
+            product(bank, *passes[0], cols, True, False)
+            product(bank, *passes[1], cols, False, True)
 
         num = sb("num", [P, PACK, S], F32)
         ksum = sb("ksum", [P, PACK, S], F32)
-        den_sq = sb("den_sq", [P, PACK, S], F32)
+        den_sq = {}
         h = [sb("h%d" % t, [P, S], F32) for t in range(PACK)]
         near = [sb("near%d" % t, [P, 2, S], F32) for t in range(PACK)]
         diff = [sb("diff%d" % t, [P, 2, S], F32) for t in range(PACK)]
@@ -271,21 +270,25 @@ def tile_picked_joinlifthopgkern_none_po_kernel(
                 gather(engine, near[t][:, b, cols], h[t], near_lists[b][:, lcols])
 
         def differences(t):
-            both = h[t][:].unsqueeze(1).to_broadcast([P, 2, S])
-            nc.vector.tensor_tensor(diff[t][:], near[t][:], both, ALU.subtract)
+            for b in range(2):
+                nc.vector.tensor_tensor(diff[t][:, b, :], near[t][:, b, :], h[t][:], ALU.subtract)
 
         def kernels(t):
-            nc.scalar.activation(sq[t][:], diff[t][:], ACT.Square)
-            nc.scalar.activation(kern[t][:], sq[t][:], ACT.Exp, scale=-0.5)
+            for b in range(2):
+                nc.scalar.activation(sq[t][:, b, :], diff[t][:, b, :], ACT.Square)
+            for b in range(2):
+                nc.scalar.activation(kern[t][:, b, :], sq[t][:, b, :], ACT.Exp, scale=-0.5)
 
         def sums(t):
             weighted = sb("weighted%d" % t, [P, 2, S], F32)
-            nc.vector.tensor_tensor(weighted[:], kern[t][:], near[t][:], ALU.mult)
+            nc.vector.tensor_tensor(weighted[:, 0, :], kern[t][:, 0, :], near[t][:, 0, :], ALU.mult)
             nc.vector.tensor_tensor(ksum[:, t, :], kern[t][:, 0, :], kern[t][:, 1, :], ALU.add)
+            nc.vector.tensor_tensor(weighted[:, 1, :], kern[t][:, 1, :], near[t][:, 1, :], ALU.mult)
             nc.vector.tensor_tensor(num[:, t, :], weighted[:, 0, :], weighted[:, 1, :], ALU.add)
 
         def square_den(t):
-            nc.scalar.activation(den_sq[:, t, :], ksum[:, t, :], ACT.Square, bias=0.5)
+            den_sq[t] = sb("den_sq%d" % t, [P, S], F32, "den_sq%d" % (t % 2))
+            nc.scalar.activation(den_sq[t][:], ksum[:, t, :], ACT.Square, bias=0.5)
 
         nc.scalar.copy(out=h[0][:, halves[0]], in_=h_first[0][:])
         nc.vector.tensor_copy(out=h[0][:, halves[1]], in_=h_first[1][:])
@@ -301,17 +304,17 @@ def tile_picked_joinlifthopgkern_none_po_kernel(
         fetch_near(nc.vector, 2, 0)
         fetch_near(nc.vector, 2, 1)
         differences(2)
+        nc.scalar.copy(out=h[3][:], in_=h_banks[3][:])
         kernels(1)
         sums(0)
-        nc.scalar.copy(out=h[3][:], in_=h_banks[3][:])
         fetch_near(nc.scalar, 3, 1)
         fetch_near(nc.vector, 3, 0)
         differences(3)
         kernels(2)
         sums(1)
+        square_den(0)
         kernels(3)
         sums(2)
-        square_den(0)
         square_den(1)
         sums(3)
 
@@ -319,9 +322,10 @@ def tile_picked_joinlifthopgkern_none_po_kernel(
         res = sb("res", [P, PACK, S], F32)
         out_rows = out_0.rearrange("(p t) c -> p t c", t=PACK)
         for t in range(PACK):
-            if t >= 2:
-                square_den(t)
-            nc.scalar.activation(recip[:, t, :], den_sq[:, t, :], ACT.Abs_reciprocal_sqrt)
+            if t == 2:
+                square_den(2)
+                square_den(3)
+            nc.scalar.activation(recip[:, t, :], den_sq[t][:], ACT.Abs_reciprocal_sqrt)
             nc.vector.tensor_tensor(res[:, t, :], num[:, t, :], recip[:, t, :], ALU.mult)
             nc.sync.dma_start(out_rows[:, t, :], res[:, t, :])
 

@@ -61,13 +61,13 @@ def tile_picked_joinlifthopgkern_none_po_kernel(
             )
             return dealt
 
-        def product(out, words, scales, t, codes, code_scales, cols, start, stop):
+        def product(out, words, scales, t, codes, code_scales, start, stop):
             nc.tensor.matmul_mx(
                 out=out,
                 lhsT=words[:, 2 * P * t : 2 * P * (t + 1)].bitcast(FP4X4),
                 lhsT_scale=scales[:, P * t : P * (t + 1)],
-                rhs=codes[:, cols].bitcast(FP8X4),
-                rhs_scale=code_scales[:, cols],
+                rhs=codes.bitcast(FP8X4),
+                rhs_scale=code_scales,
                 start=start,
                 stop=stop,
             )
@@ -105,10 +105,8 @@ def tile_picked_joinlifthopgkern_none_po_kernel(
         nc.scalar.dma_start(w1w_raw[:].bitcast(I32), w1_words[0].bitcast(I32))
         xw_all = sb("xw_all", [P, T], U32)
         nc.sync.dma_start(xw_all[:].bitcast(I32), x_words[0].rearrange("p n t -> p (n t)").bitcast(I32))
-        load_scale_rows(nc.scalar, w1s_raw, w1_scales, 0)
-        load_scale_rows(nc.scalar, w1s_raw, w1_scales, 1)
-        load_scale_rows(nc.gpsimd, w1s_raw, w1_scales, 2)
-        load_scale_rows(nc.gpsimd, w1s_raw, w1_scales, 3)
+        for q in range(4):
+            load_scale_rows(nc.scalar, w1s_raw, w1_scales, q)
         n1_sb = load_list("n1_sb", n1)
         n2_sb = load_list("n2_sb", n2)
         n3_sb = load_list("n3_sb", n3)
@@ -132,16 +130,17 @@ def tile_picked_joinlifthopgkern_none_po_kernel(
         xs = sb("xs", [P, S], U8)
         nc.vector.tensor_copy(xs[:], xs_all[:].indirect(offs_sb[:]))
         w1s = deal_scales("w1s", w1s_raw)
-        xw = sb("xw", [P, S], U32, "xs_all")
-        for cols, lcols in zip(halves, list_halves):
-            nc.vector.tensor_copy(xw[:, cols], xw_all[:].indirect(offs_sb[:, lcols]))
+        xw = [sb("xw0", [P, HALF], U32, "xs_all"), sb("xw1", [P, HALF], U32, "w1s_raw")]
+        for u in range(2):
+            nc.vector.tensor_copy(xw[u][:], xw_all[:].indirect(offs_sb[:, list_halves[u]]))
 
         y_first = [psum.tile([P, HALF], F32, name="y_first%d" % u, tag="bank%d" % u) for u in range(2)]
         y_banks = [None] + [psum.tile([P, S], F32, name="y_bank%d" % t, tag="bank%d" % (t + 1)) for t in range(1, PACK)]
         for u in range(2):
-            product(y_first[u][:], w1w, w1s, 0, xw, xs, halves[u], True, True)
+            product(y_first[u][:], w1w, w1s, 0, xw[u][:], xs[:, halves[u]], True, True)
         for t in range(1, PACK):
-            product(y_banks[t][:], w1w, w1s, t, xw, xs, slice(0, S), True, True)
+            for u in range(2):
+                product(y_banks[t][:, halves[u]], w1w, w1s, t, xw[u][:], xs[:, halves[u]], True, True)
 
         z_planes = sb("z_planes", [P, PACK * S], BF16)
         z2_planes = sb("z2_planes", [P, PACK * S], BF16)
@@ -150,7 +149,7 @@ def tile_picked_joinlifthopgkern_none_po_kernel(
         def plane(planes, t):
             return planes[:, S * t : S * (t + 1)]
 
-        y = [sb("y%d" % t, [P, S], F32) for t in range(PACK)]
+        y = [sb("y%d" % t, [P, S], F32, "xw1" if t == 1 else None) for t in range(PACK)]
         gate = [sb("gate%d" % t, [P, S], F32) for t in range(PACK)]
         hop = [sb("hop%d" % t, [P, S], F32) for t in range(PACK)]
         st = [sb("st%d" % t, [P, S], F32) for t in range(PACK)]
@@ -244,34 +243,39 @@ def tile_picked_joinlifthopgkern_none_po_kernel(
             quantise(z2_codes, z2_scales, z2_woven, cols)
 
         h_first = [psum.tile([P, HALF], F32, name="h_first%d" % u, tag="bank%d" % (5 + u)) for u in range(2)]
-        h_tags = [None, "bank5", "bank6", "bank6"]
+        h_tags = [None, "bank7", "bank0", "bank1"]
         h_banks = [None] + [psum.tile([P, S], F32, name="h_bank%d" % t, tag=h_tags[t]) for t in range(1, PACK)]
         groups = [(h_first[u][:], 0, halves[u]) for u in range(2)]
         groups.extend((h_banks[t][:], t, slice(0, S)) for t in range(1, PACK))
         for bank, t, cols in groups:
-            passes = [(w3w, w3s, t, z2_codes, z2_scales), (w2w, w2s, t, z_codes, z_scales)]
+            passes = [
+                (w3w, w3s, t, z2_codes[:, cols], z2_scales[:, cols]),
+                (w2w, w2s, t, z_codes[:, cols], z_scales[:, cols]),
+            ]
             if t == 0:
                 passes = passes[::-1]
-            product(bank, *passes[0], cols, True, False)
-            product(bank, *passes[1], cols, False, True)
+            product(bank, *passes[0], True, False)
+            product(bank, *passes[1], False, True)
 
         num = sb("num", [P, PACK, S], F32)
-        ksum = sb("ksum", [P, PACK, S], F32)
+        ksum = {}
         den_sq = {}
         h = [sb("h%d" % t, [P, S], F32) for t in range(PACK)]
-        near = [sb("near%d" % t, [P, 2, S], F32) for t in range(PACK)]
+        near = {t: sb("near%d" % t, [P, 2, S], F32) for t in range(last)}
         diff = [sb("diff%d" % t, [P, 2, S], F32) for t in range(PACK)]
         sq = [sb("sq%d" % t, [P, 2, S], F32) for t in range(PACK)]
         kern = [sb("kern%d" % t, [P, 2, S], F32) for t in range(PACK)]
         near_lists = [n5_sb, n6_sb]
 
-        def fetch_near(engine, t, b):
-            for cols, lcols in zip(halves, list_halves):
-                gather(engine, near[t][:, b, cols], h[t], near_lists[b][:, lcols])
+        def fetch_near(engine, t, b, which=(0, 1)):
+            for u in which:
+                gather(engine, near[t][:, b, halves[u]], h[t], near_lists[b][:, list_halves[u]])
 
-        def differences(t):
-            for b in range(2):
-                nc.vector.tensor_tensor(diff[t][:, b, :], near[t][:, b, :], h[t][:], ALU.subtract)
+        def difference(t, b):
+            if t < 2:
+                nc.gpsimd.tensor_tensor(diff[t][:, b, :], near[t][:, b, :], h[t][:], ALU.subtract)
+            else:
+                nc.vector.tensor_tensor(diff[t][:, b, :], near[t][:, b, :], h_banks[t][:], ALU.subtract)
 
         def kernels(t):
             for b in range(2):
@@ -282,34 +286,47 @@ def tile_picked_joinlifthopgkern_none_po_kernel(
         def sums(t):
             weighted = sb("weighted%d" % t, [P, 2, S], F32)
             nc.vector.tensor_tensor(weighted[:, 0, :], kern[t][:, 0, :], near[t][:, 0, :], ALU.mult)
-            nc.vector.tensor_tensor(ksum[:, t, :], kern[t][:, 0, :], kern[t][:, 1, :], ALU.add)
-            nc.vector.tensor_tensor(weighted[:, 1, :], kern[t][:, 1, :], near[t][:, 1, :], ALU.mult)
-            nc.vector.tensor_tensor(num[:, t, :], weighted[:, 0, :], weighted[:, 1, :], ALU.add)
+            if t == 0:
+                nc.vector.tensor_tensor(weighted[:, 1, :], kern[t][:, 1, :], near[t][:, 1, :], ALU.mult)
+                ksum[t] = sb("ksum%d" % t, [P, S], F32, "near0")
+                nc.gpsimd.tensor_tensor(ksum[t][:], kern[t][:, 0, :], kern[t][:, 1, :], ALU.add)
+                nc.gpsimd.tensor_tensor(num[:, t, :], weighted[:, 0, :], weighted[:, 1, :], ALU.add)
+            else:
+                ksum[t] = sb("ksum%d" % t, [P, S], F32)
+                nc.vector.tensor_tensor(ksum[t][:], kern[t][:, 0, :], kern[t][:, 1, :], ALU.add)
+                nc.vector.tensor_tensor(weighted[:, 1, :], kern[t][:, 1, :], near[t][:, 1, :], ALU.mult)
+                nc.vector.tensor_tensor(num[:, t, :], weighted[:, 0, :], weighted[:, 1, :], ALU.add)
 
         def square_den(t):
             den_sq[t] = sb("den_sq%d" % t, [P, S], F32, "den_sq%d" % (t % 2))
-            nc.scalar.activation(den_sq[t][:], ksum[:, t, :], ACT.Square, bias=0.5)
+            nc.scalar.activation(den_sq[t][:], ksum[t][:], ACT.Square, bias=0.5)
 
         nc.scalar.copy(out=h[0][:, halves[0]], in_=h_first[0][:])
         nc.vector.tensor_copy(out=h[0][:, halves[1]], in_=h_first[1][:])
-        fetch_near(nc.vector, 0, 0)
+        fetch_near(nc.vector, 0, 0, [0])
+        nc.vector.tensor_copy(out=h[1][:], in_=h_banks[1][:])
+        fetch_near(nc.vector, 0, 0, [1])
         fetch_near(nc.scalar, 0, 1)
-        nc.scalar.copy(out=h[1][:], in_=h_banks[1][:])
-        differences(0)
+        difference(0, 0)
+        difference(0, 1)
+        nc.scalar.copy(out=h[2][:], in_=h_banks[2][:])
         fetch_near(nc.vector, 1, 0)
         fetch_near(nc.scalar, 1, 1)
-        nc.vector.tensor_copy(out=h[2][:], in_=h_banks[2][:])
-        differences(1)
-        kernels(0)
-        fetch_near(nc.vector, 2, 0)
-        fetch_near(nc.vector, 2, 1)
-        differences(2)
+        difference(1, 0)
+        difference(1, 1)
         nc.scalar.copy(out=h[3][:], in_=h_banks[3][:])
-        kernels(1)
+        kernels(0)
+        for b in range(2):
+            fetch_near(nc.vector, 2, b)
+        for b in range(2):
+            difference(2, b)
         sums(0)
+        near[3] = sb("near3", [P, 2, S], F32, "sq0")
         fetch_near(nc.scalar, 3, 1)
         fetch_near(nc.vector, 3, 0)
-        differences(3)
+        difference(3, 0)
+        difference(3, 1)
+        kernels(1)
         kernels(2)
         sums(1)
         square_den(0)
@@ -325,18 +342,18 @@ def tile_picked_joinlifthopgkern_none_po_kernel(
             if t == 2:
                 square_den(2)
                 square_den(3)
-            nc.scalar.activation(recip[:, t, :], den_sq[t][:], ACT.Abs_reciprocal_sqrt)
-            nc.vector.tensor_tensor(res[:, t, :], num[:, t, :], recip[:, t, :], ALU.mult)
+            for cols in halves if t == last else [slice(0, S)]:
+                nc.scalar.activation(recip[:, t, cols], den_sq[t][:, cols], ACT.Abs_reciprocal_sqrt)
+                nc.vector.tensor_tensor(res[:, t, cols], num[:, t, cols], recip[:, t, cols], ALU.mult)
             nc.sync.dma_start(out_rows[:, t, :], res[:, t, :])
 
         o_woven = sb("o_woven", [P, S, PACK], BF16)
         o_codes = sb("o_codes", [P, S], U32)
         o_scales = sb("o_scales", [P, S], U8)
-        weave(nc.vector, o_woven, res, halves[0])
-        weave(nc.scalar, o_woven, res, slice(3 * S // 4, S))
-        weave(nc.vector, o_woven, res, slice(HALF, 3 * S // 4))
+        weave(nc.scalar, o_woven, res, halves[0])
+        weave(nc.vector, o_woven, res, halves[1])
         out_words = out_1[0].rearrange("p n t -> p (n t)").bitcast(I32)
-        for cols in halves:
+        for cols in halves[::-1]:
             quantise(o_codes, o_scales, o_woven, cols)
             nc.sync.dma_start(out_words[:, cols], o_codes[:, cols].bitcast(I32))
         for q in range(4):

@@ -242,6 +242,9 @@ def tile_picked_joinlifthopgkern_none_po_kernel(
             quantise(z_codes, z_scales, z_woven, cols)
             quantise(z2_codes, z2_scales, z2_woven, cols)
 
+        warm = sb("warm", [P, 1], F32, "z2_planes")
+        nc.scalar.activation(warm[:], gm_sb[:, 0:1], ACT.Exp, scale=0.0)
+
         h_first = [psum.tile([P, HALF], F32, name="h_first%d" % u, tag="bank%d" % (5 + u)) for u in range(2)]
         h_tags = [None, "bank7", "bank0", "bank1"]
         h_banks = [None] + [psum.tile([P, S], F32, name="h_bank%d" % t, tag=h_tags[t]) for t in range(1, PACK)]

@@ -15,9 +15,12 @@ ALU = mybir.AluOpType
 
 P = 128
 PACK = 4
+LAST = PACK - 1
+QUADRANTS = 4
 T = 2048
 S = 512
 HALF = S // 2
+ENTRIES_PER_COLUMN = 16
 FLOPS = 3 * 2 * 512 * 512 * 512
 
 
@@ -26,35 +29,46 @@ def tile_picked_joinlifthopgkern_none_po_kernel(
     offs, n1, n2, n3, n4, n5, n6, out_0, out_1, out_2,
 ):
     nc = tc.nc
+    whole = slice(0, S)
     halves = [slice(0, HALF), slice(HALF, S)]
-    list_halves = [slice(0, HALF // 16), slice(HALF // 16, S // 16)]
+    list_halves = [slice(h.start // ENTRIES_PER_COLUMN, h.stop // ENTRIES_PER_COLUMN) for h in halves]
 
     with ExitStack() as ctx:
         keep = ctx.enter_context(tc.tile_pool(name="keep", bufs=1))
         psum = ctx.enter_context(tc.psum_pool(name="psum", bufs=1))
 
-        def sb(name, shape, dtype, tag=None):
-            return keep.tile(shape, dtype, name=name, tag=tag or name, align_bytes=64)
+        def sb(name, shape, dtype, after=None):
+            return keep.tile(shape, dtype, name=name, tag=after or name, align_bytes=64)
 
         def load_list(name, src):
             tile = sb(name, list(src.shape), U16)
             nc.sync.dma_start(tile[:], src)
             return tile
 
-        def load_scale_rows(queue, tile_cols, src, q):
-            rows = src[0, 4 * q : 4 * q + 4, :].bitcast(I32).partition_broadcast(8)
-            queue.dma_start(tile_cols[32 * q : 32 * q + 32, :].bitcast(I32), rows)
+        def load_gains(name, src):
+            tile = sb(name, [P, PACK], F32)
+            nc.sync.dma_start(tile[:], src.rearrange("(p t) o -> p (t o)", t=PACK))
+            return tile
 
-        def deal_words(name, raw, tag=None):
-            dealt = sb(name, [P, 2 * S], U8, tag)
+        def load_weight_words(queue, name, src):
+            tile = sb(name, [P, 2 * S], U8)
+            queue.dma_start(tile[:].bitcast(I32), src[0].bitcast(I32))
+            return tile
+
+        def load_scale_rows(queue, tile, src, q):
+            rows = src[0, 4 * q : 4 * q + 4, :].bitcast(I32).partition_broadcast(8)
+            queue.dma_start(tile[32 * q : 32 * q + 32, :].bitcast(I32), rows)
+
+        def deal_words(name, raw, after):
+            dealt = sb(name, [P, 2 * S], U8, after)
             nc.scalar.copy(
                 out=dealt[:].bitcast(U16).rearrange("p (t m) -> p t m", t=PACK),
                 in_=raw[:].bitcast(U16).rearrange("p (m t) -> p t m", t=PACK),
             )
             return dealt
 
-        def deal_scales(name, raw, tag=None):
-            dealt = sb(name, [P, S], U8, tag)
+        def deal_scales(name, raw, after=None):
+            dealt = sb(name, [P, S], U8, after)
             nc.vector.tensor_copy(
                 out=dealt[:].rearrange("p (t m) -> p t m", t=PACK),
                 in_=raw[:].rearrange("p (m t) -> p t m", t=PACK),
@@ -97,45 +111,42 @@ def tile_picked_joinlifthopgkern_none_po_kernel(
         xs_all = sb("xs_all", [P, T], U8)
         w2s_raw = sb("w2s_raw", [P, S], U8)
         w3s_raw = sb("w3s_raw", [P, S], U8)
-
         offs_sb = load_list("offs_sb", offs)
-        for q in range(4):
-            load_scale_rows(nc.sync if q < 2 else nc.scalar, xs_all, x_scales, q)
-        w1w_raw = sb("w1w_raw", [P, 2 * S], U8)
-        nc.scalar.dma_start(w1w_raw[:].bitcast(I32), w1_words[0].bitcast(I32))
+        for q in range(QUADRANTS):
+            load_scale_rows(nc.sync if q < QUADRANTS // 2 else nc.scalar, xs_all, x_scales, q)
+        w1w_raw = load_weight_words(nc.scalar, "w1w_raw", w1_words)
         xw_all = sb("xw_all", [P, T], U32)
-        nc.sync.dma_start(xw_all[:].bitcast(I32), x_words[0].rearrange("p n t -> p (n t)").bitcast(I32))
-        for q in range(4):
-            load_scale_rows(nc.scalar, w1s_raw, w1_scales, q)
+        nc.scalar.dma_start(xw_all[:].bitcast(I32), x_words[0].rearrange("p n t -> p (n t)").bitcast(I32))
+        for q in range(QUADRANTS):
+            load_scale_rows(nc.sync, w1s_raw, w1_scales, q)
         n1_sb = load_list("n1_sb", n1)
         n2_sb = load_list("n2_sb", n2)
         n3_sb = load_list("n3_sb", n3)
-        gm_sb = sb("gm_sb", [P, PACK], F32)
-        nc.sync.dma_start(gm_sb[:], gm.rearrange("(p t) o -> p (t o)", t=PACK))
+        gm_sb = load_gains("gm_sb", gm)
         n4_sb = load_list("n4_sb", n4)
-        for q in range(4):
-            load_scale_rows(nc.sync, w3s_raw, w3_scales, q)
-        w3w_raw = sb("w3w_raw", [P, 2 * S], U8)
-        nc.sync.dma_start(w3w_raw[:].bitcast(I32), w3_words[0].bitcast(I32))
-        gn_sb = sb("gn_sb", [P, PACK], F32)
-        nc.sync.dma_start(gn_sb[:], gn.rearrange("(p t) o -> p (t o)", t=PACK))
-        w2w_raw = sb("w2w_raw", [P, 2 * S], U8)
-        nc.sync.dma_start(w2w_raw[:].bitcast(I32), w2_words[0].bitcast(I32))
-        for q in range(4):
-            load_scale_rows(nc.sync, w2s_raw, w2_scales, q)
+        for raw, src in ((w3s_raw, w3_scales), (w2s_raw, w2_scales)):
+            for q in range(QUADRANTS):
+                load_scale_rows(nc.sync, raw, src, q)
+        gn_sb = load_gains("gn_sb", gn)
+        w3w_raw = load_weight_words(nc.sync, "w3w_raw", w3_words)
+        w2w_raw = load_weight_words(nc.sync, "w2w_raw", w2_words)
         n5_sb = load_list("n5_sb", n5)
         n6_sb = load_list("n6_sb", n6)
 
-        w1w = deal_words("w1w", w1w_raw)
         xs = sb("xs", [P, S], U8)
         nc.vector.tensor_copy(xs[:], xs_all[:].indirect(offs_sb[:]))
+        w1w = sb("w1w", [P, 2 * S], U8, after="xs_all")
+        nc.vector.tensor_copy(
+            out=w1w[:].rearrange("p (t m b) -> p t m b", t=PACK, b=2),
+            in_=w1w_raw[:].rearrange("p (m t b) -> p t m b", t=PACK, b=2),
+        )
         w1s = deal_scales("w1s", w1s_raw)
-        xw = [sb("xw0", [P, HALF], U32, "xs_all"), sb("xw1", [P, HALF], U32, "w1s_raw")]
+        xw = [sb("xw0", [P, HALF], U32, after="w1w_raw"), sb("xw1", [P, HALF], U32, after="w1s_raw")]
         for u in range(2):
             nc.vector.tensor_copy(xw[u][:], xw_all[:].indirect(offs_sb[:, list_halves[u]]))
 
         y_first = [psum.tile([P, HALF], F32, name="y_first%d" % u, tag="bank%d" % u) for u in range(2)]
-        y_banks = [None] + [psum.tile([P, S], F32, name="y_bank%d" % t, tag="bank%d" % (t + 1)) for t in range(1, PACK)]
+        y_banks = {t: psum.tile([P, S], F32, name="y_bank%d" % t, tag="bank%d" % (t + 1)) for t in range(1, PACK)}
         for u in range(2):
             product(y_first[u][:], w1w, w1s, 0, xw[u][:], xs[:, halves[u]], True, True)
         for t in range(1, PACK):
@@ -144,50 +155,60 @@ def tile_picked_joinlifthopgkern_none_po_kernel(
 
         z_planes = sb("z_planes", [P, PACK * S], BF16)
         z2_planes = sb("z2_planes", [P, PACK * S], BF16)
-        last = PACK - 1
 
         def plane(planes, t):
             return planes[:, S * t : S * (t + 1)]
 
-        y = [sb("y%d" % t, [P, S], F32, "xw1" if t == 1 else None) for t in range(PACK)]
+        y = [sb("y%d" % t, [P, S], F32, after="w1s_raw" if t == 1 else None) for t in range(PACK)]
         gate = [sb("gate%d" % t, [P, S], F32) for t in range(PACK)]
         hop = [sb("hop%d" % t, [P, S], F32) for t in range(PACK)]
         st = [sb("st%d" % t, [P, S], F32) for t in range(PACK)]
-        rb = [sb("rb%d" % t, [P, HALF], F32) for t in range(PACK)]
+        rb = [sb("rb%d" % t, [P, HALF], F32, after="w2s_raw" if t == 2 else None) for t in range(PACK)]
         neg_pa0 = sb("neg_pa0", [P, HALF], F32)
         pb0 = sb("pb0", [P, HALF], F32)
-        neg_pa = [neg_pa0[:], plane(z_planes, 0).bitcast(F32), plane(z2_planes, 2).bitcast(F32), plane(z_planes, 1).bitcast(F32)]
-        pb = [pb0[:], plane(z2_planes, 0).bitcast(F32), plane(z2_planes, 1).bitcast(F32), plane(z2_planes, 3).bitcast(F32)]
+        neg_pa3 = sb("neg_pa3", [P, HALF], F32)
+        neg_pa = [neg_pa0[:], plane(z_planes, 0).bitcast(F32), plane(z2_planes, 2).bitcast(F32), neg_pa3[:]]
+        pb = [pb0[:]] + [plane(z2_planes, t).bitcast(F32) for t in (0, 1, 3)]
         dt = {}
 
-        def put_pairs(t, tag=None):
+        def put_ra(t, after=None):
             nc.vector.scalar_tensor_tensor(rb[t][:], neg_pa[t], -0.5, pb[t], ALU.mult, ALU.max)
-            dt[t] = sb("dt%d" % t, [P, S], F32, tag)
+            dt[t] = sb("dt%d" % t, [P, S], F32, after)
             nc.vector.tensor_tensor(dt[t][:].indirect(n1_sb[:]), pb[t], neg_pa[t], ALU.add)
 
         def put_rb(t):
             nc.vector.tensor_copy(dt[t][:].indirect(n2_sb[:]), rb[t][:])
 
-        def fetch_pairs(t, tag=None):
+        def fetch_gate(t, u):
+            nc.scalar.activation(gate[t][:, halves[u]], y[t][:].indirect(n3_sb[:, list_halves[u]]), ACT.Sigmoid)
+
+        def lift(t, gated_plane=None, after=None):
             nc.scalar.activation(neg_pa[t], y[t][:].indirect(n1_sb[:]), ACT.Copy, scale=-1.0)
+            if gated_plane is not None:
+                fetch_gate(gated_plane, 0)
             gather(nc.scalar, pb[t], y[t], n2_sb[:])
-            put_pairs(t, tag)
+            put_ra(t, after)
+            if gated_plane is not None:
+                fetch_gate(gated_plane, 1)
+                make_st(gated_plane, whole, y_banks[gated_plane][:])
             put_rb(t)
 
-        def make_st(cols, t, bank):
-            nc.vector.scalar_tensor_tensor(st[t][:, cols], bank, gm_sb[:, t : t + 1], gate[t][:, cols], ALU.mult, ALU.mult)
+        def make_st(t, cols, bank):
+            nc.vector.scalar_tensor_tensor(
+                st[t][:, cols], bank, gm_sb[:, t : t + 1], gate[t][:, cols], ALU.mult, ALU.mult
+            )
 
-        def fetch_gate(t):
-            for cols, lcols in zip(halves, list_halves):
-                nc.scalar.activation(gate[t][:, cols], y[t][:].indirect(n3_sb[:, lcols]), ACT.Sigmoid)
-            make_st(slice(0, S), t, y_banks[t][:])
+        def gated(t):
+            for u in range(2):
+                fetch_gate(t, u)
+            make_st(t, whole, y_banks[t][:])
 
-        def fetch_hop(t):
+        def make_z2(t):
             for cols, lcols in zip(halves, list_halves):
                 gather(nc.scalar, hop[t][:, cols], st[t], n4_sb[:, lcols])
             nc.gpsimd.tensor_tensor(plane(z2_planes, t), st[t][:], hop[t][:], ALU.subtract)
 
-        def gain(t, engine):
+        def make_z(t, engine):
             if engine is nc.scalar:
                 nc.scalar.activation(plane(z_planes, t), dt[t][:], ACT.Copy, scale=gn_sb[:, t : t + 1])
             else:
@@ -199,33 +220,32 @@ def tile_picked_joinlifthopgkern_none_po_kernel(
         nc.vector.tensor_copy(out=y[0][:, halves[1]], in_=y_first[1][:])
         nc.vector.tensor_scalar(neg_pa[0], y[0][:].indirect(n1_sb[:]), -1.0, 0.0, ALU.mult, ALU.add)
         gather(nc.scalar, pb[0], y[0], n2_sb[:])
-        put_pairs(0)
-        w3s = deal_scales("w3s", w3s_raw, "neg_pa0")
-        w2s = deal_scales("w2s", w2s_raw, "pb0")
+        put_ra(0)
         put_rb(0)
         nc.scalar.activation(sig0[:, halves[1]], y_first[1][:], ACT.Sigmoid)
         nc.scalar.copy(out=y[1][:], in_=y_banks[1][:])
         for cols, lcols in zip(halves, list_halves):
             gather(nc.scalar, gate[0][:, cols], sig0, n3_sb[:, lcols])
         for u in range(2):
-            make_st(halves[u], 0, y_first[u][:])
-        fetch_pairs(1)
+            make_st(0, halves[u], y_first[u][:])
+
+        lift(1, gated_plane=1)
         nc.scalar.copy(out=y[2][:], in_=y_banks[2][:])
-        fetch_gate(1)
-        fetch_hop(0)
-        gain(0, nc.gpsimd)
-        fetch_gate(2)
-        fetch_pairs(2, "gate2")
+        make_z2(0)
+        make_z(0, nc.gpsimd)
+        gated(2)
+        w3s = deal_scales("w3s", w3s_raw, after="hop0")
+        w2s = deal_scales("w2s", w2s_raw, after="w3s_raw")
         nc.scalar.copy(out=y[3][:], in_=y_banks[3][:])
-        fetch_hop(1)
-        fetch_hop(2)
-        fetch_gate(3)
-        fetch_pairs(3, "gate3")
-        fetch_hop(3)
-        w3w = deal_words("w3w", w3w_raw, "hop1")
-        w2w = deal_words("w2w", w2w_raw, "hop2")
-        gain(1, nc.scalar)
-        gain(2, nc.scalar)
+        lift(2, gated_plane=3, after="gate2")
+        make_z2(1)
+        make_z2(2)
+        lift(3)
+        make_z2(3)
+        w3w = deal_words("w3w", w3w_raw, after="hop1")
+        w2w = deal_words("w2w", w2w_raw, after="hop2")
+        make_z(1, nc.scalar)
+        make_z(2, nc.scalar)
 
         z2_woven = sb("z2_woven", [P, S, PACK], BF16)
         z2_codes = sb("z2_codes", [P, S], U32)
@@ -233,40 +253,37 @@ def tile_picked_joinlifthopgkern_none_po_kernel(
         z_woven = sb("z_woven", [P, S, PACK], BF16)
         z_codes = sb("z_codes", [P, S], U32)
         z_scales = sb("z_scales", [P, S], U8)
-        gain(last, nc.vector)
+        make_z(LAST, nc.vector)
         for cols in halves:
             weave(nc.scalar, z2_woven, z2_planes[:].rearrange("p (t c) -> p t c", t=PACK), cols)
-        weave(nc.vector, z_woven, z_planes[:].rearrange("p (t c) -> p t c", t=PACK), slice(0, HALF))
-        weave(nc.vector, z_woven, z_planes[:].rearrange("p (t c) -> p t c", t=PACK), slice(HALF, S))
+        for cols in halves:
+            weave(nc.vector, z_woven, z_planes[:].rearrange("p (t c) -> p t c", t=PACK), cols)
         for cols in halves:
             quantise(z_codes, z_scales, z_woven, cols)
             quantise(z2_codes, z2_scales, z2_woven, cols)
 
-        warm = sb("warm", [P, 1], F32, "z2_planes")
+        warm = sb("warm", [P, 1], F32, after="z2_planes")
         nc.scalar.activation(warm[:], gm_sb[:, 0:1], ACT.Exp, scale=0.0)
 
-        h_first = [psum.tile([P, HALF], F32, name="h_first%d" % u, tag="bank%d" % (5 + u)) for u in range(2)]
-        h_tags = [None, "bank7", "bank0", "bank1"]
-        h_banks = [None] + [psum.tile([P, S], F32, name="h_bank%d" % t, tag=h_tags[t]) for t in range(1, PACK)]
+        h_first = [psum.tile([P, HALF], F32, name="h_first%d" % u, tag="bank%d" % (PACK + 1 + u)) for u in range(2)]
+        h_tags = {1: "bank7", 2: "bank0", 3: "bank1"}
+        h_banks = {t: psum.tile([P, S], F32, name="h_bank%d" % t, tag=h_tags[t]) for t in range(1, PACK)}
         groups = [(h_first[u][:], 0, halves[u]) for u in range(2)]
-        groups.extend((h_banks[t][:], t, slice(0, S)) for t in range(1, PACK))
+        groups.extend((h_banks[t][:], t, whole) for t in range(1, PACK))
         for bank, t, cols in groups:
-            passes = [
-                (w3w, w3s, t, z2_codes[:, cols], z2_scales[:, cols]),
-                (w2w, w2s, t, z_codes[:, cols], z_scales[:, cols]),
-            ]
-            if t == 0:
-                passes = passes[::-1]
-            product(bank, *passes[0], True, False)
-            product(bank, *passes[1], False, True)
+            z_pass = (w2w, w2s, t, z_codes[:, cols], z_scales[:, cols])
+            z2_pass = (w3w, w3s, t, z2_codes[:, cols], z2_scales[:, cols])
+            opening, closing = (z_pass, z2_pass) if t == 0 else (z2_pass, z_pass)
+            product(bank, *opening, True, False)
+            product(bank, *closing, False, True)
 
         num = sb("num", [P, PACK, S], F32)
         ksum = {}
         den_sq = {}
-        h = [sb("h%d" % t, [P, S], F32) for t in range(PACK)]
-        near = {t: sb("near%d" % t, [P, 2, S], F32) for t in range(last)}
+        h = [sb("h%d" % t, [P, S], F32, after="z2_woven" if t == 0 else None) for t in range(PACK)]
+        near = {t: sb("near%d" % t, [P, 2, S], F32) for t in range(LAST)}
         diff = [sb("diff%d" % t, [P, 2, S], F32) for t in range(PACK)]
-        sq = [sb("sq%d" % t, [P, 2, S], F32) for t in range(PACK)]
+        sq = {}
         kern = [sb("kern%d" % t, [P, 2, S], F32) for t in range(PACK)]
         near_lists = [n5_sb, n6_sb]
 
@@ -274,81 +291,96 @@ def tile_picked_joinlifthopgkern_none_po_kernel(
             for u in which:
                 gather(engine, near[t][:, b, halves[u]], h[t], near_lists[b][:, list_halves[u]])
 
-        def difference(t, b):
-            if t < 2:
-                nc.gpsimd.tensor_tensor(diff[t][:, b, :], near[t][:, b, :], h[t][:], ALU.subtract)
-            else:
-                nc.vector.tensor_tensor(diff[t][:, b, :], near[t][:, b, :], h_banks[t][:], ALU.subtract)
+        def differences(t, engine):
+            own = h[t][:] if engine is nc.gpsimd else h_banks[t][:]
+            for b in range(2):
+                engine.tensor_tensor(diff[t][:, b, :], near[t][:, b, :], own, ALU.subtract)
 
-        def kernels(t):
+        def kernels(t, after=None):
+            sq[t] = sb("sq%d" % t, [P, 2, S], F32, after)
             for b in range(2):
                 nc.scalar.activation(sq[t][:, b, :], diff[t][:, b, :], ACT.Square)
             for b in range(2):
                 nc.scalar.activation(kern[t][:, b, :], sq[t][:, b, :], ACT.Exp, scale=-0.5)
 
+        def weigh(weighted, t, b):
+            nc.vector.tensor_tensor(weighted[:, b, :], kern[t][:, b, :], near[t][:, b, :], ALU.mult)
+
+        def sums_on_gpsimd(t):
+            weighted = sb("weighted%d" % t, [P, 2, S], F32)
+            for b in range(2):
+                weigh(weighted, t, b)
+            ksum[t] = sb("ksum%d" % t, [P, S], F32, after="near%d" % t)
+            nc.gpsimd.tensor_tensor(ksum[t][:], kern[t][:, 0, :], kern[t][:, 1, :], ALU.add)
+            nc.gpsimd.tensor_tensor(num[:, t, :], weighted[:, 0, :], weighted[:, 1, :], ALU.add)
+
         def sums(t):
             weighted = sb("weighted%d" % t, [P, 2, S], F32)
-            nc.vector.tensor_tensor(weighted[:, 0, :], kern[t][:, 0, :], near[t][:, 0, :], ALU.mult)
-            if t == 0:
-                nc.vector.tensor_tensor(weighted[:, 1, :], kern[t][:, 1, :], near[t][:, 1, :], ALU.mult)
-                ksum[t] = sb("ksum%d" % t, [P, S], F32, "near0")
-                nc.gpsimd.tensor_tensor(ksum[t][:], kern[t][:, 0, :], kern[t][:, 1, :], ALU.add)
-                nc.gpsimd.tensor_tensor(num[:, t, :], weighted[:, 0, :], weighted[:, 1, :], ALU.add)
-            else:
-                ksum[t] = sb("ksum%d" % t, [P, S], F32)
-                nc.vector.tensor_tensor(ksum[t][:], kern[t][:, 0, :], kern[t][:, 1, :], ALU.add)
-                nc.vector.tensor_tensor(weighted[:, 1, :], kern[t][:, 1, :], near[t][:, 1, :], ALU.mult)
-                nc.vector.tensor_tensor(num[:, t, :], weighted[:, 0, :], weighted[:, 1, :], ALU.add)
+            weigh(weighted, t, 0)
+            ksum[t] = sb("ksum%d" % t, [P, S], F32)
+            nc.vector.tensor_tensor(ksum[t][:], kern[t][:, 0, :], kern[t][:, 1, :], ALU.add)
+            weigh(weighted, t, 1)
+            nc.vector.tensor_tensor(num[:, t, :], weighted[:, 0, :], weighted[:, 1, :], ALU.add)
 
-        def square_den(t):
-            den_sq[t] = sb("den_sq%d" % t, [P, S], F32, "den_sq%d" % (t % 2))
+        def last_sums(t):
+            weighted = sb("weighted%d" % t, [P, 2, S], F32)
+            weigh(weighted, t, 0)
+            den = sb("den%d" % t, [P, S], F32)
+            nc.vector.scalar_tensor_tensor(den[:], kern[t][:, 0, :], 0.5, kern[t][:, 1, :], ALU.add, ALU.add)
+            weigh(weighted, t, 1)
+            den_sq[t] = sb("den_sq%d" % t, [P, S], F32)
+            nc.vector.tensor_tensor(den_sq[t][:], den[:], den[:], ALU.mult)
+            nc.vector.tensor_tensor(num[:, t, :], weighted[:, 0, :], weighted[:, 1, :], ALU.add)
+
+        def square_den(t, after=None):
+            den_sq[t] = sb("den_sq%d" % t, [P, S], F32, after)
             nc.scalar.activation(den_sq[t][:], ksum[t][:], ACT.Square, bias=0.5)
 
-        nc.scalar.copy(out=h[0][:, halves[0]], in_=h_first[0][:])
-        nc.vector.tensor_copy(out=h[0][:, halves[1]], in_=h_first[1][:])
-        fetch_near(nc.vector, 0, 0, [0])
-        nc.vector.tensor_copy(out=h[1][:], in_=h_banks[1][:])
-        fetch_near(nc.vector, 0, 0, [1])
-        fetch_near(nc.scalar, 0, 1)
-        difference(0, 0)
-        difference(0, 1)
+        for u in range(2):
+            nc.vector.tensor_copy(out=h[0][:, halves[u]], in_=h_first[u][:])
+        fetch_near(nc.vector, 0, 0)
+        fetch_near(nc.scalar, 0, 1, [0])
+        nc.scalar.copy(out=h[1][:], in_=h_banks[1][:])
+        fetch_near(nc.scalar, 0, 1, [1])
+        differences(0, nc.gpsimd)
         nc.scalar.copy(out=h[2][:], in_=h_banks[2][:])
         fetch_near(nc.vector, 1, 0)
         fetch_near(nc.scalar, 1, 1)
-        difference(1, 0)
-        difference(1, 1)
+        differences(1, nc.gpsimd)
         nc.scalar.copy(out=h[3][:], in_=h_banks[3][:])
         kernels(0)
         for b in range(2):
             fetch_near(nc.vector, 2, b)
-        for b in range(2):
-            difference(2, b)
-        sums(0)
-        near[3] = sb("near3", [P, 2, S], F32, "sq0")
+        differences(2, nc.vector)
+        sums_on_gpsimd(0)
+        near[3] = sb("near3", [P, 2, S], F32, after="sq0")
         fetch_near(nc.scalar, 3, 1)
         fetch_near(nc.vector, 3, 0)
-        difference(3, 0)
-        difference(3, 1)
+        differences(3, nc.vector)
         kernels(1)
-        kernels(2)
+        kernels(2, after="diff1")
         sums(1)
         square_den(0)
         kernels(3)
         sums(2)
         square_den(1)
-        sums(3)
+        last_sums(LAST)
 
-        recip = sb("recip", [P, PACK, S], F32, "sq%d" % last)
+        recip = sb("recip", [P, PACK, S], F32, after="sq%d" % LAST)
         res = sb("res", [P, PACK, S], F32)
         out_rows = out_0.rearrange("(p t) c -> p t c", t=PACK)
-        for t in range(PACK):
-            if t == 2:
-                square_den(2)
-                square_den(3)
-            for cols in halves if t == last else [slice(0, S)]:
+
+        def divide(t):
+            for cols in halves if t == LAST else [whole]:
                 nc.scalar.activation(recip[:, t, cols], den_sq[t][:, cols], ACT.Abs_reciprocal_sqrt)
                 nc.vector.tensor_tensor(res[:, t, cols], num[:, t, cols], recip[:, t, cols], ALU.mult)
             nc.sync.dma_start(out_rows[:, t, :], res[:, t, :])
+
+        divide(0)
+        divide(1)
+        square_den(2, after="den_sq0")
+        divide(2)
+        divide(LAST)
 
         o_woven = sb("o_woven", [P, S, PACK], BF16)
         o_codes = sb("o_codes", [P, S], U32)
@@ -359,6 +391,6 @@ def tile_picked_joinlifthopgkern_none_po_kernel(
         for cols in halves[::-1]:
             quantise(o_codes, o_scales, o_woven, cols)
             nc.sync.dma_start(out_words[:, cols], o_codes[:, cols].bitcast(I32))
-        for q in range(4):
+        for q in range(QUADRANTS):
             queue = nc.sync if q % 2 == 0 else nc.scalar
             queue.dma_start(out_2[0, 4 * q : 4 * q + 4, :].bitcast(I32), o_scales[32 * q : 32 * q + 4, :].bitcast(I32))

from contextlib import ExitStack

import concourse.mybir as mybir

F32 = mybir.dt.float32
BF16 = mybir.dt.bfloat16
I32 = mybir.dt.int32
U32 = mybir.dt.uint32
U16 = mybir.dt.uint16
U8 = mybir.dt.uint8
FP8X4 = mybir.dt.float8_e4m3fn_x4
FP4X4 = mybir.dt.float4_e2m1fn_x4
ACT = mybir.ActivationFunctionType
ALU = mybir.AluOpType

P = 128
PACK = 4
LAST = PACK - 1
QUADRANTS = 4
T = 2048
S = 512
HALF = S // 2
ENTRIES_PER_COLUMN = 16
FLOPS = 3 * 2 * 512 * 512 * 512


def tile_picked_joinlifthopgkern_none_po_kernel(
    tc, x_words, x_scales, w1_words, w1_scales, gn, gm, w2_words, w2_scales, w3_words, w3_scales,
    offs, n1, n2, n3, n4, n5, n6, out_0, out_1, out_2,
):
    nc = tc.nc
    whole = slice(0, S)
    halves = [slice(0, HALF), slice(HALF, S)]
    list_halves = [slice(h.start // ENTRIES_PER_COLUMN, h.stop // ENTRIES_PER_COLUMN) for h in halves]

    with ExitStack() as ctx:
        keep = ctx.enter_context(tc.tile_pool(name="keep", bufs=1))
        psum = ctx.enter_context(tc.psum_pool(name="psum", bufs=1))

        def sb(name, shape, dtype, after=None):
            return keep.tile(shape, dtype, name=name, tag=after or name, align_bytes=64)

        def load_list(name, src):
            tile = sb(name, list(src.shape), U16)
            nc.sync.dma_start(tile[:], src)
            return tile

        def load_gains(name, src):
            tile = sb(name, [P, PACK], F32)
            nc.sync.dma_start(tile[:], src.rearrange("(p t) o -> p (t o)", t=PACK))
            return tile

        def load_weight_words(queue, name, src):
            tile = sb(name, [P, 2 * S], U8)
            queue.dma_start(tile[:].bitcast(I32), src[0].bitcast(I32))
            return tile

        def load_scale_rows(queue, tile, src, q):
            rows = src[0, 4 * q : 4 * q + 4, :].bitcast(I32).partition_broadcast(8)
            queue.dma_start(tile[32 * q : 32 * q + 32, :].bitcast(I32), rows)

        def deal_words(name, raw, after):
            dealt = sb(name, [P, 2 * S], U8, after)
            nc.scalar.copy(
                out=dealt[:].bitcast(U16).rearrange("p (t m) -> p t m", t=PACK),
                in_=raw[:].bitcast(U16).rearrange("p (m t) -> p t m", t=PACK),
            )
            return dealt

        def deal_scales(name, raw, after=None):
            dealt = sb(name, [P, S], U8, after)
            nc.vector.tensor_copy(
                out=dealt[:].rearrange("p (t m) -> p t m", t=PACK),
                in_=raw[:].rearrange("p (m t) -> p t m", t=PACK),
            )
            return dealt

        def product(out, words, scales, t, codes, code_scales, start, stop):
            nc.tensor.matmul_mx(
                out=out,
                lhsT=words[:, 2 * P * t : 2 * P * (t + 1)].bitcast(FP4X4),
                lhsT_scale=scales[:, P * t : P * (t + 1)],
                rhs=codes.bitcast(FP8X4),
                rhs_scale=code_scales,
                start=start,
                stop=stop,
            )

        def gather(engine, out, window, offsets):
            if engine is nc.vector:
                nc.vector.tensor_copy(out, window[:].indirect(offsets))
            else:
                nc.scalar.activation(out, window[:].indirect(offsets), ACT.Copy)

        def weave(engine, woven, planes, cols):
            dst = woven[:, cols, :].rearrange("p (c i) t -> p c t i", i=4)
            src = planes[:, :, cols].rearrange("p t (c i) -> p c t i", i=4)
            if engine is nc.vector:
                nc.vector.tensor_copy(out=dst, in_=src)
            else:
                nc.scalar.copy(out=dst, in_=src)

        def quantise(codes, scales, woven, cols):
            nc.vector.quantize_mx(
                out=codes[:, cols].bitcast(FP8X4),
                scales=scales[:, cols],
                in_=woven[:, cols, :].rearrange("p c t -> p (c t)"),
            )

        w1s_raw = sb("w1s_raw", [P, S], U8)
        xs_all = sb("xs_all", [P, T], U8)
        w2s_raw = sb("w2s_raw", [P, S], U8)
        w3s_raw = sb("w3s_raw", [P, S], U8)
        offs_sb = load_list("offs_sb", offs)
        for q in range(QUADRANTS):
            load_scale_rows(nc.sync if q < QUADRANTS // 2 else nc.scalar, xs_all, x_scales, q)
        w1w_raw = load_weight_words(nc.scalar, "w1w_raw", w1_words)
        xw_all = sb("xw_all", [P, T], U32)
        nc.scalar.dma_start(xw_all[:].bitcast(I32), x_words[0].rearrange("p n t -> p (n t)").bitcast(I32))
        for q in range(QUADRANTS):
            load_scale_rows(nc.sync, w1s_raw, w1_scales, q)
        n1_sb = load_list("n1_sb", n1)
        n2_sb = load_list("n2_sb", n2)
        n3_sb = load_list("n3_sb", n3)
        gm_sb = load_gains("gm_sb", gm)
        n4_sb = load_list("n4_sb", n4)
        for raw, src in ((w3s_raw, w3_scales), (w2s_raw, w2_scales)):
            for q in range(QUADRANTS):
                load_scale_rows(nc.sync, raw, src, q)
        gn_sb = load_gains("gn_sb", gn)
        w3w_raw = load_weight_words(nc.sync, "w3w_raw", w3_words)
        w2w_raw = load_weight_words(nc.sync, "w2w_raw", w2_words)
        n5_sb = load_list("n5_sb", n5)
        n6_sb = load_list("n6_sb", n6)

        xs = sb("xs", [P, S], U8)
        nc.vector.tensor_copy(xs[:], xs_all[:].indirect(offs_sb[:]))
        w1w = sb("w1w", [P, 2 * S], U8, after="xs_all")
        nc.vector.tensor_copy(
            out=w1w[:].rearrange("p (t m b) -> p t m b", t=PACK, b=2),
            in_=w1w_raw[:].rearrange("p (m t b) -> p t m b", t=PACK, b=2),
        )
        w1s = deal_scales("w1s", w1s_raw)
        xw = [sb("xw0", [P, HALF], U32, after="w1w_raw"), sb("xw1", [P, HALF], U32, after="w1s_raw")]
        for u in range(2):
            nc.vector.tensor_copy(xw[u][:], xw_all[:].indirect(offs_sb[:, list_halves[u]]))

        y_first = [psum.tile([P, HALF], F32, name="y_first%d" % u, tag="bank%d" % u) for u in range(2)]
        y_banks = {t: psum.tile([P, S], F32, name="y_bank%d" % t, tag="bank%d" % (t + 1)) for t in range(1, PACK)}
        for u in range(2):
            product(y_first[u][:], w1w, w1s, 0, xw[u][:], xs[:, halves[u]], True, True)
        for t in range(1, PACK):
            for u in range(2):
                product(y_banks[t][:, halves[u]], w1w, w1s, t, xw[u][:], xs[:, halves[u]], True, True)

        z_planes = sb("z_planes", [P, PACK * S], BF16)
        z2_planes = sb("z2_planes", [P, PACK * S], BF16)

        def plane(planes, t):
            return planes[:, S * t : S * (t + 1)]

        y = [sb("y%d" % t, [P, S], F32, after="w1s_raw" if t == 1 else None) for t in range(PACK)]
        gate = [sb("gate%d" % t, [P, S], F32) for t in range(PACK)]
        hop = [sb("hop%d" % t, [P, S], F32) for t in range(PACK)]
        st = [sb("st%d" % t, [P, S], F32) for t in range(PACK)]
        rb = [sb("rb%d" % t, [P, HALF], F32, after="w2s_raw" if t == 2 else None) for t in range(PACK)]
        neg_pa0 = sb("neg_pa0", [P, HALF], F32)
        pb0 = sb("pb0", [P, HALF], F32)
        neg_pa3 = sb("neg_pa3", [P, HALF], F32)
        neg_pa = [neg_pa0[:], plane(z_planes, 0).bitcast(F32), plane(z2_planes, 2).bitcast(F32), neg_pa3[:]]
        pb = [pb0[:]] + [plane(z2_planes, t).bitcast(F32) for t in (0, 1, 3)]
        dt = {}

        def put_ra(t, after=None):
            nc.vector.scalar_tensor_tensor(rb[t][:], neg_pa[t], -0.5, pb[t], ALU.mult, ALU.max)
            dt[t] = sb("dt%d" % t, [P, S], F32, after)
            nc.vector.tensor_tensor(dt[t][:].indirect(n1_sb[:]), pb[t], neg_pa[t], ALU.add)

        def put_rb(t):
            nc.vector.tensor_copy(dt[t][:].indirect(n2_sb[:]), rb[t][:])

        def fetch_gate(t, u):
            nc.scalar.activation(gate[t][:, halves[u]], y[t][:].indirect(n3_sb[:, list_halves[u]]), ACT.Sigmoid)

        def lift(t, gated_plane=None, after=None):
            nc.scalar.activation(neg_pa[t], y[t][:].indirect(n1_sb[:]), ACT.Copy, scale=-1.0)
            if gated_plane is not None:
                fetch_gate(gated_plane, 0)
            gather(nc.scalar, pb[t], y[t], n2_sb[:])
            put_ra(t, after)
            if gated_plane is not None:
                fetch_gate(gated_plane, 1)
                make_st(gated_plane, whole, y_banks[gated_plane][:])
            put_rb(t)

        def make_st(t, cols, bank):
            nc.vector.scalar_tensor_tensor(
                st[t][:, cols], bank, gm_sb[:, t : t + 1], gate[t][:, cols], ALU.mult, ALU.mult
            )

        def gated(t):
            for u in range(2):
                fetch_gate(t, u)
            make_st(t, whole, y_banks[t][:])

        def make_z2(t):
            for cols, lcols in zip(halves, list_halves):
                gather(nc.scalar, hop[t][:, cols], st[t], n4_sb[:, lcols])
            nc.gpsimd.tensor_tensor(plane(z2_planes, t), st[t][:], hop[t][:], ALU.subtract)

        def make_z(t, engine):
            if engine is nc.scalar:
                nc.scalar.activation(plane(z_planes, t), dt[t][:], ACT.Copy, scale=gn_sb[:, t : t + 1])
            else:
                engine.tensor_scalar(plane(z_planes, t), dt[t][:], gn_sb[:, t : t + 1], 0.0, ALU.mult, ALU.add)

        sig0 = sb("sig0", [P, S], F32)
        nc.scalar.activation(sig0[:, halves[0]], y_first[0][:], ACT.Sigmoid)
        nc.scalar.copy(out=y[0][:, halves[0]], in_=y_first[0][:])
        nc.vector.tensor_copy(out=y[0][:, halves[1]], in_=y_first[1][:])
        nc.vector.tensor_scalar(neg_pa[0], y[0][:].indirect(n1_sb[:]), -1.0, 0.0, ALU.mult, ALU.add)
        gather(nc.scalar, pb[0], y[0], n2_sb[:])
        put_ra(0)
        put_rb(0)
        nc.scalar.activation(sig0[:, halves[1]], y_first[1][:], ACT.Sigmoid)
        nc.scalar.copy(out=y[1][:], in_=y_banks[1][:])
        for cols, lcols in zip(halves, list_halves):
            gather(nc.scalar, gate[0][:, cols], sig0, n3_sb[:, lcols])
        for u in range(2):
            make_st(0, halves[u], y_first[u][:])

        lift(1, gated_plane=1)
        nc.scalar.copy(out=y[2][:], in_=y_banks[2][:])
        make_z2(0)
        make_z(0, nc.gpsimd)
        gated(2)
        w3s = deal_scales("w3s", w3s_raw, after="hop0")
        w2s = deal_scales("w2s", w2s_raw, after="w3s_raw")
        nc.scalar.copy(out=y[3][:], in_=y_banks[3][:])
        lift(2, gated_plane=3, after="gate2")
        make_z2(1)
        make_z2(2)
        lift(3)
        make_z2(3)
        w3w = deal_words("w3w", w3w_raw, after="hop1")
        w2w = deal_words("w2w", w2w_raw, after="hop2")
        make_z(1, nc.scalar)
        make_z(2, nc.scalar)

        z2_woven = sb("z2_woven", [P, S, PACK], BF16)
        z2_codes = sb("z2_codes", [P, S], U32)
        z2_scales = sb("z2_scales", [P, S], U8)
        z_woven = sb("z_woven", [P, S, PACK], BF16)
        z_codes = sb("z_codes", [P, S], U32)
        z_scales = sb("z_scales", [P, S], U8)
        make_z(LAST, nc.vector)
        for cols in halves:
            weave(nc.scalar, z2_woven, z2_planes[:].rearrange("p (t c) -> p t c", t=PACK), cols)
        for cols in halves:
            weave(nc.vector, z_woven, z_planes[:].rearrange("p (t c) -> p t c", t=PACK), cols)
        for cols in halves:
            quantise(z_codes, z_scales, z_woven, cols)
            quantise(z2_codes, z2_scales, z2_woven, cols)

        warm = sb("warm", [P, 1], F32, after="z2_planes")
        nc.scalar.activation(warm[:], gm_sb[:, 0:1], ACT.Exp, scale=0.0)

        h_first = [psum.tile([P, HALF], F32, name="h_first%d" % u, tag="bank%d" % (PACK + 1 + u)) for u in range(2)]
        h_tags = {1: "bank7", 2: "bank0", 3: "bank1"}
        h_banks = {t: psum.tile([P, S], F32, name="h_bank%d" % t, tag=h_tags[t]) for t in range(1, PACK)}
        groups = [(h_first[u][:], 0, halves[u]) for u in range(2)]
        groups.extend((h_banks[t][:], t, whole) for t in range(1, PACK))
        for bank, t, cols in groups:
            z_pass = (w2w, w2s, t, z_codes[:, cols], z_scales[:, cols])
            z2_pass = (w3w, w3s, t, z2_codes[:, cols], z2_scales[:, cols])
            opening, closing = (z_pass, z2_pass) if t == 0 else (z2_pass, z_pass)
            product(bank, *opening, True, False)
            product(bank, *closing, False, True)

        num = sb("num", [P, PACK, S], F32)
        ksum = {}
        den_sq = {}
        h = [sb("h%d" % t, [P, S], F32, after="z2_woven" if t == 0 else None) for t in range(PACK)]
        near = {t: sb("near%d" % t, [P, 2, S], F32) for t in range(LAST)}
        diff = [sb("diff%d" % t, [P, 2, S], F32) for t in range(PACK)]
        sq = {}
        kern = [sb("kern%d" % t, [P, 2, S], F32) for t in range(PACK)]
        near_lists = [n5_sb, n6_sb]

        def fetch_near(engine, t, b, which=(0, 1)):
            for u in which:
                gather(engine, near[t][:, b, halves[u]], h[t], near_lists[b][:, list_halves[u]])

        def differences(t, engine):
            own = h[t][:] if engine is nc.gpsimd else h_banks[t][:]
            for b in range(2):
                engine.tensor_tensor(diff[t][:, b, :], near[t][:, b, :], own, ALU.subtract)

        def kernels(t, after=None):
            sq[t] = sb("sq%d" % t, [P, 2, S], F32, after)
            for b in range(2):
                nc.scalar.activation(sq[t][:, b, :], diff[t][:, b, :], ACT.Square)
            for b in range(2):
                nc.scalar.activation(kern[t][:, b, :], sq[t][:, b, :], ACT.Exp, scale=-0.5)

        def weigh(weighted, t, b):
            nc.vector.tensor_tensor(weighted[:, b, :], kern[t][:, b, :], near[t][:, b, :], ALU.mult)

        def sums_on_gpsimd(t):
            weighted = sb("weighted%d" % t, [P, 2, S], F32)
            for b in range(2):
                weigh(weighted, t, b)
            ksum[t] = sb("ksum%d" % t, [P, S], F32, after="near%d" % t)
            nc.gpsimd.tensor_tensor(ksum[t][:], kern[t][:, 0, :], kern[t][:, 1, :], ALU.add)
            nc.gpsimd.tensor_tensor(num[:, t, :], weighted[:, 0, :], weighted[:, 1, :], ALU.add)

        def sums(t):
            weighted = sb("weighted%d" % t, [P, 2, S], F32)
            weigh(weighted, t, 0)
            ksum[t] = sb("ksum%d" % t, [P, S], F32)
            nc.vector.tensor_tensor(ksum[t][:], kern[t][:, 0, :], kern[t][:, 1, :], ALU.add)
            weigh(weighted, t, 1)
            nc.vector.tensor_tensor(num[:, t, :], weighted[:, 0, :], weighted[:, 1, :], ALU.add)

        def last_sums(t):
            weighted = sb("weighted%d" % t, [P, 2, S], F32)
            weigh(weighted, t, 0)
            den = sb("den%d" % t, [P, S], F32)
            nc.vector.scalar_tensor_tensor(den[:], kern[t][:, 0, :], 0.5, kern[t][:, 1, :], ALU.add, ALU.add)
            weigh(weighted, t, 1)
            den_sq[t] = sb("den_sq%d" % t, [P, S], F32)
            nc.vector.tensor_tensor(den_sq[t][:], den[:], den[:], ALU.mult)
            nc.vector.tensor_tensor(num[:, t, :], weighted[:, 0, :], weighted[:, 1, :], ALU.add)

        def square_den(t, after=None):
            den_sq[t] = sb("den_sq%d" % t, [P, S], F32, after)
            nc.scalar.activation(den_sq[t][:], ksum[t][:], ACT.Square, bias=0.5)

        for u in range(2):
            nc.vector.tensor_copy(out=h[0][:, halves[u]], in_=h_first[u][:])
        fetch_near(nc.vector, 0, 0)
        fetch_near(nc.scalar, 0, 1, [0])
        nc.scalar.copy(out=h[1][:], in_=h_banks[1][:])
        fetch_near(nc.scalar, 0, 1, [1])
        differences(0, nc.gpsimd)
        nc.scalar.copy(out=h[2][:], in_=h_banks[2][:])
        fetch_near(nc.vector, 1, 0)
        fetch_near(nc.scalar, 1, 1)
        differences(1, nc.gpsimd)
        nc.scalar.copy(out=h[3][:], in_=h_banks[3][:])
        kernels(0)
        for b in range(2):
            fetch_near(nc.vector, 2, b)
        differences(2, nc.vector)
        sums_on_gpsimd(0)
        near[3] = sb("near3", [P, 2, S], F32, after="sq0")
        fetch_near(nc.scalar, 3, 1)
        fetch_near(nc.vector, 3, 0)
        differences(3, nc.vector)
        kernels(1)
        kernels(2, after="diff1")
        sums(1)
        square_den(0)
        kernels(3)
        sums(2)
        square_den(1)
        last_sums(LAST)

        recip = sb("recip", [P, PACK, S], F32, after="sq%d" % LAST)
        res = sb("res", [P, PACK, S], F32)
        out_rows = out_0.rearrange("(p t) c -> p t c", t=PACK)

        def divide(t):
            for cols in halves if t == LAST else [whole]:
                nc.scalar.activation(recip[:, t, cols], den_sq[t][:, cols], ACT.Abs_reciprocal_sqrt)
                nc.vector.tensor_tensor(res[:, t, cols], num[:, t, cols], recip[:, t, cols], ALU.mult)
            nc.sync.dma_start(out_rows[:, t, :], res[:, t, :])

        divide(0)
        divide(1)
        square_den(2, after="den_sq0")
        divide(2)
        divide(LAST)

        o_woven = sb("o_woven", [P, S, PACK], BF16)
        o_codes = sb("o_codes", [P, S], U32)
        o_scales = sb("o_scales", [P, S], U8)
        weave(nc.scalar, o_woven, res, halves[0])
        weave(nc.vector, o_woven, res, halves[1])
        out_words = out_1[0].rearrange("p n t -> p (n t)").bitcast(I32)
        for cols in halves[::-1]:
            quantise(o_codes, o_scales, o_woven, cols)
            nc.sync.dma_start(out_words[:, cols], o_codes[:, cols].bitcast(I32))
        for q in range(QUADRANTS):
            queue = nc.sync if q % 2 == 0 else nc.scalar
            queue.dma_start(out_2[0, 4 * q : 4 * q + 4, :].bitcast(I32), o_scales[32 * q : 32 * q + 4, :].bitcast(I32))
